import numpy as np
import ml_dtypes


def mxq(x, axis, fmt="e4m3"):
    dtype, down = {"e4m3": (ml_dtypes.float8_e4m3fn, 7), "e5m2": (ml_dtypes.float8_e5m2, 14)}[fmt]
    v = np.moveaxis(np.asarray(x, np.float32).astype(ml_dtypes.bfloat16).astype(np.float64), axis, -1)
    blocks = v.reshape(v.shape[:-1] + (-1, 32))
    amax = np.abs(blocks).max(-1, keepdims=True)
    byte = np.maximum(np.where(amax > 0, np.frexp(amax)[1] - 1 + 127, 0) - down, 1)
    scale = np.exp2(byte - 127.0)
    codes = (blocks / scale).astype(np.float32).astype(dtype).astype(np.float64)
    return np.moveaxis((codes * scale).reshape(v.shape), -1, axis)


WIDE = False


def mx_kscale(k):
    if not WIDE:
        return np.ones(k)
    levels = np.array([10, -10, 5, -5, 0])
    if k % 512:
        return np.exp2(np.random.permutation(np.resize(levels, k // 32))).repeat(32)
    a = np.empty((k // 512, 16))
    for p in range(k // 512):
        a[p, :8] = np.random.permutation(np.resize(levels, 8))
        for g in range(8):
            far = levels[np.abs(levels - a[p, g]) >= 10]
            a[p, g + 8] = far[np.random.randint(len(far))]
    return np.exp2(a.ravel()).repeat(32)


def f64(x):
    return np.asarray(x).astype(np.float64)


def striped(idx):
    return np.tile(idx.reshape(-1, 16).T, (8, 1)).astype(np.uint16)


def unstriped(offs):
    return offs[:16].T.reshape(-1).astype(np.int64)


E2M1 = np.array([0.0, 0.5, 1.0, 1.5, 2.0, 3.0, 4.0, 6.0, -0.0, -0.5, -1.0, -1.5, -2.0, -3.0, -4.0, -6.0])


def pack_weight(w, fmt):
    k, n = w.shape
    w = f64(np.asarray(w, np.float32).astype(ml_dtypes.bfloat16)).reshape(k // 32, 32, n)
    amax = np.abs(w).max(1)
    if fmt == "e4m3":
        byte = np.frexp(amax)[1] - 1 + 127 - 7
    else:
        mant, ex = np.frexp(amax / 6.0)
        byte = np.where(mant > 0.5, ex, ex - 1) + 127
    byte = np.clip(np.where(amax > 0, byte, 1), 1, 254)
    scaled = (w * np.exp2(127.0 - byte)[:, None, :]).reshape(k, n).astype(np.float32)
    by_word = np.ascontiguousarray(scaled.reshape(k // 512, 128, 4, n).transpose(0, 1, 3, 2))
    if fmt == "e4m3":
        words = by_word.astype(ml_dtypes.float8_e4m3fn).view(np.uint8)
    else:
        c = by_word.astype(ml_dtypes.float4_e2m1fn).view(np.uint8) & 0xF
        words = (c[..., 0::2] | (c[..., 1::2] << 4)).reshape(k // 512, 128, 2 * n)
    return np.ascontiguousarray(words), np.ascontiguousarray(byte.astype(np.uint8).reshape(k // 512, 16, n))


def unpack_weight(words, scales, fmt):
    g, _, n = scales.shape
    words = np.ascontiguousarray(words).reshape(g, 128, n, -1)
    if fmt == "e4m3":
        vals = words.view(ml_dtypes.float8_e4m3fn).astype(np.float64)
    else:
        nib = np.empty((g, 128, n, 4), np.uint8)
        nib[..., 0::2] = words & 0xF
        nib[..., 1::2] = words >> 4
        vals = E2M1[nib]
    vals = vals * np.repeat(np.exp2(scales.astype(np.float64) - 127.0), 8, axis=1)[..., None]
    return vals.transpose(0, 1, 3, 2).reshape(g * 512, n)


def gelu(v):
    return 0.5 * v * (1.0 + np.tanh(np.sqrt(2.0 / np.pi) * (v + 0.044715 * v**3)))


def bf(x):
    return np.asarray(x, np.float32).astype(ml_dtypes.bfloat16)


def planes(Y):
    n, m = Y.shape
    b = f64(bf(Y)).reshape(n // 32, 32, m)
    amax = np.abs(b).max(1)
    byte = np.clip(np.where(amax > 0, np.frexp(amax)[1] - 1 + 127 - 7, 1), 1, 254)
    codes = (b * np.exp2(127.0 - byte)[:, None, :]).reshape(n, m).astype(np.float32).astype(ml_dtypes.float8_e4m3fn).view(np.uint8)
    words = codes.reshape(n // 512, 128, 4, m).transpose(0, 1, 3, 2)
    return np.ascontiguousarray(words), np.ascontiguousarray(byte.astype(np.uint8).reshape(n // 512, 16, m))


K, H, N, T, S, T2 = 1024, 1024, 256, 2048, 1024, 2048

def setup_inputs():
    n = np.random.standard_normal
    s = mx_kscale(K)[:, None]
    u = mx_kscale(H)[:, None]
    tab_words, tab_scales = pack_weight(n((K, T)) * s, "e4m3")
    wa4_words, wa4_scales = pack_weight(n((H, N)) / np.sqrt(H) / u, "e2m1")
    return {
        "tab_words": tab_words, "tab_scales": tab_scales,
        "offs": striped(np.random.permutation(T)[:S]),
        "w1": (1.5 * n((K, H)) / np.sqrt(K) / s).astype(np.float32),
        "gain": (np.exp(0.3 * n(H)) * u[:, 0]).astype(np.float32),
        "page0": (n((H, T2)) * u).astype(np.float32),
        "offs2": striped(np.random.permutation(T2)[:S]),
        "wgs": np.exp(0.3 * n((128, S))).astype(np.float32),
        "wa4_words": wa4_words, "wa4_scales": wa4_scales,
        "wb": (n((H, N)) / np.sqrt(H) / u).astype(np.float32),
    }

def reference(tab_words, tab_scales, offs, w1, gain, page0, offs2, wgs, wa4_words, wa4_scales, wb):
    v = unpack_weight(tab_words, tab_scales, "e4m3")[:, unstriped(offs)]
    x = mxq(f64(w1), 0, "e4m3").T @ v
    h = np.log(1.0 + np.square(x)) * f64(gain)[:, None]
    page = f64(page0).copy()
    page[:, unstriped(offs2)] = np.tile(f64(wgs), (H // 128, 1)) * h
    pq = mxq(page, 0, "e4m3")
    ya = unpack_weight(wa4_words, wa4_scales, "e2m1").T @ pq
    yb = mxq(f64(wb), 0, "e4m3").T @ pq
    y = np.maximum(ya, yb)
    words, scales = planes(page)
    return y, page, words, scales

@@ -1,0 +1,379 @@
+from contextlib import ExitStack
+
+import concourse.mybir as mybir
+
+K, H, N, T, S, T2 = 1024, 1024, 256, 2048, 1024, 2048
+FLOPS = 2 * K * H * S + 2 * 2 * H * N * T2
+
+F32 = mybir.dt.float32
+BF16 = mybir.dt.bfloat16
+I32 = mybir.dt.int32
+U32 = mybir.dt.uint32
+U16 = mybir.dt.uint16
+U8 = mybir.dt.uint8
+FP8X4 = mybir.dt.float8_e4m3fn_x4
+FP4X4 = mybir.dt.float4_e2m1fn_x4
+ACT = mybir.ActivationFunctionType
+ALU = mybir.AluOpType
+
+P = 128
+PACK = 4
+KP = P * PACK
+BANK = 512
+PASSES = K // KP
+GROUPS = H // KP
+CHUNKS = T2 // BANK
+QUADS = 4
+HALF = S // 2
+
+
+def tile_list_cyclist_tile_page_kernel(
+    tc, tab_words, tab_scales, offs, w1, gain, page0, offs2, wgs, wa4_words, wa4_scales, wb,
+    out_0, out_1, out_2, out_3,
+):
+    nc = tc.nc
+    with ExitStack() as ctx:
+        keep = ctx.enter_context(tc.tile_pool(name="keep", bufs=1))
+        ring = ctx.enter_context(tc.tile_pool(name="ring", bufs=4))
+        psum = ctx.enter_context(tc.psum_pool(name="psum", bufs=8))
+
+        def held(shape, dtype, name):
+            return keep.tile(shape, dtype, name=name, align_bytes=64)
+
+        def rotating(shape, dtype, name, tag):
+            return ring.tile(shape, dtype, name=name, tag=tag, align_bytes=64)
+
+        offs_sb = keep.tile([P, S // 16], U16, name="offs_sb")
+        offs2_sb = keep.tile([P, S // 16], U16, name="offs2_sb")
+        tabw = keep.tile([P, PASSES * T], U32, name="tabw", tag="wide", align_bytes=64)
+        tabs = held([P, T], U8, "tabs")
+        vw = [held([P, S], U32, f"vw{a}") for a in range(PASSES)]
+        vs = held([P, S], U8, "vs")
+        gain_sb = held([P, GROUPS, PACK], F32, "gain_sb")
+        wg_first = held([P, S], F32, "wg_first")
+        wg_rest = keep.tile([P, (PACK - 1) * S], F32, name="wg_rest", tag="wg_rest", align_bytes=64)
+        wg = [wg_first[:]] + [wg_rest[:, S * t : S * (t + 1)] for t in range(PACK - 1)]
+        page = [[held([P, T2], F32, f"page{g}{t}") for t in range(PACK)] for g in range(GROUPS)]
+        w1c = [[held([P, KP], U32, f"w1c{g}{a}") for a in range(PASSES)] for g in range(GROUPS)]
+        w1s = [[held([P, KP], U8, f"w1s{g}{a}") for a in range(PASSES)] for g in range(GROUPS)]
+        pc = [held([P, T2], U32, f"pc{g}") for g in range(GROUPS)]
+        ps = [held([P, T2], U8, f"ps{g}") for g in range(GROUPS)]
+        wb_raw = held([P, GROUPS, PACK * N], F32, "wb_raw")
+        wbs = held([P, GROUPS * N], U8, "wbs")
+        waw = held([P, GROUPS, 2 * N], U8, "waw")
+        was = held([P, GROUPS, N], U8, "was")
+        warm = held([P, 2], F32, "warm")
+
+        nc.vector.memset(warm[:, 0:1], 1.0)
+        nc.scalar.activation(out=warm[:, 1:2], in_=warm[:, 0:1], func=ACT.Ln)
+
+        nc.vector.memset(tabs[:].bitcast(I32), 0)
+        for q in range(QUADS):
+            nc.scalar.dma_start(
+                out=tabs[32 * q : 32 * q + 4 * PASSES, :].bitcast(I32),
+                in_=tab_scales[:, 4 * q : 4 * q + 4, :].bitcast(I32),
+            )
+        nc.vector.memset(was[:].rearrange("p g n -> p (g n)").bitcast(I32), 0)
+
+        page_in = page0.rearrange("(g p t) c -> g t p c", g=GROUPS, t=PACK)
+        page_out = out_1.rearrange("(g p t) c -> g t p c", g=GROUPS, t=PACK)
+        wgs_rows = wgs.rearrange("(m t) j -> m (t j)", t=PACK)
+        w1_raw = {}
+
+        def load_words(a):
+            nc.sync.dma_start(
+                out=tabw[:, T * a : T * (a + 1)].bitcast(I32), in_=tab_words[a].rearrange("p n i -> p (n i)").bitcast(I32)
+            )
+
+        def load_w1(g, a):
+            raw = keep.tile([P, PACK, KP], F32, name=f"w1raw{g}{a}", tag=f"raw{g}{a}", align_bytes=64)
+            rows = w1[KP * a : KP * (a + 1), KP * g : KP * (g + 1)]
+            nc.sync.dma_start(out=raw[:], in_=rows.rearrange("(p j) c -> p j c", j=PACK))
+            w1_raw[(g, a)] = raw
+
+        def load_wgs(tile, cols):
+            for q in (0, 2, 1, 3):
+                nc.sync.dma_start(out=tile[32 * q : 32 * (q + 1), :], in_=wgs_rows[:, cols])
+
+        def load_page(g, t):
+            nc.sync.dma_start(out=page[g][t][:], in_=page_in[g, t])
+
+        nc.sync.dma_start(offs_sb[:], offs)
+        nc.sync.dma_start(offs2_sb[:], offs2)
+        nc.sync.dma_start(out=gain_sb[:], in_=gain.rearrange("(g p t) -> p g t", g=GROUPS, t=PACK))
+        nc.sync.dma_start(out=waw[:].bitcast(I32), in_=wa4_words.rearrange("g p c -> p g c").bitcast(I32))
+        load_words(0)
+        load_w1(0, 0)
+        load_w1(0, 1)
+        load_words(1)
+        load_page(0, 0)
+        load_wgs(wg_first, slice(0, S))
+        load_page(0, 1)
+        load_wgs(wg_rest, slice(S, PACK * S))
+        load_w1(1, 0)
+        load_w1(1, 1)
+        load_page(0, 2)
+        load_page(0, 3)
+        nc.sync.dma_start(out=wb_raw[:], in_=wb.rearrange("(g p j) n -> p g (j n)", g=GROUPS, j=PACK))
+        for q in range(QUADS):
+            nc.sync.dma_start(
+                out=was[32 * q : 32 * q + 4, :, :].bitcast(I32),
+                in_=wa4_scales[:, 4 * q : 4 * q + 4, :].rearrange("g r n -> r g n").bitcast(I32),
+            )
+        for t in range(PACK):
+            load_page(1, t)
+
+        def copy_on(engine, out, in_):
+            if engine == "vector":
+                nc.vector.tensor_copy(out=out, in_=in_)
+            else:
+                nc.scalar.copy(out=out, in_=in_)
+
+        def cast_w1(g, a, engines):
+            st = rotating([P, KP * PACK], BF16, f"w1st{g}{a}", "stage")
+            share = P // len(engines)
+            for i, engine in enumerate(engines):
+                ms = slice(share * i, share * (i + 1))
+                copy_on(
+                    engine,
+                    st[:].rearrange("p (t m j) -> p m j t", t=PACK, j=PACK)[:, ms],
+                    w1_raw[(g, a)][:].rearrange("p j (m t) -> p m j t", t=PACK)[:, ms],
+                )
+            nc.vector.quantize_mx(out=w1c[g][a][:].bitcast(FP8X4), scales=w1s[g][a][:], in_=st[:])
+
+        def gather_words(a, lo, hi):
+            nc.vector.tensor_copy(out=vw[a][:, lo:hi], in_=tabw[:, T * a : T * (a + 1)].indirect(offs_sb[:, lo // 16 : hi // 16]))
+
+        gather_words(0, 0, S)
+        nc.vector.tensor_copy(out=vs[:], in_=tabs[:].indirect(offs_sb[:]))
+        cast_w1(0, 0, ["scalar"])
+        cast_w1(0, 1, ["scalar", "vector"])
+        first_pieces = [slice(0, S // 4), slice(S // 4, HALF), slice(HALF, S)]
+        for js in first_pieces:
+            gather_words(1, js.start, js.stop)
+
+        pair0 = keep.tile([P, PACK * T2], BF16, name="pair0", tag="wide", align_bytes=64)
+        pair0_words = pair0[:].bitcast(F32)
+        h_slot = {(0, 3): "raw11", (1, 1): "raw00", (1, 2): "raw01", (1, 3): "raw10"}
+        square_at = {(0, 3): 0, (1, 2): T2}
+        halves = [slice(0, HALF), slice(HALF, S)]
+
+        def apply_gain(g, t, out, h):
+            for js in halves:
+                nc.scalar.activation(out=out[:, js], in_=h[:, js], func=ACT.Copy, scale=gain_sb[:, g, t : t + 1])
+
+        def first_product(g, t, js):
+            cols = slice(P * t, P * (t + 1))
+            x = psum.tile([P, BANK], F32, name=f"x{g}{t}{js.start}", tag="bank")
+            x = x[:, 0 : js.stop - js.start]
+            for a in range(PASSES):
+                nc.tensor.matmul_mx(
+                    out=x,
+                    lhsT=w1c[g][a][:, cols].bitcast(FP8X4),
+                    lhsT_scale=w1s[g][a][:, cols],
+                    rhs=vw[a][:, js].bitcast(FP8X4),
+                    rhs_scale=vs[4 * a : P, js],
+                    start=(a == 0),
+                    stop=(a == PASSES - 1),
+                )
+            return x
+
+        def new_h(g, t):
+            if (g, t) in h_slot:
+                h_tile = keep.tile([P, S], F32, name=f"h{g}{t}", tag=h_slot[(g, t)], align_bytes=64)
+            else:
+                h_tile = rotating([P, S], F32, f"h{g}{t}", "h")
+            return h_tile[:]
+
+        def make_h(g, t, h, with_gain=True):
+            sq = pair0_words[:, square_at[(g, t)] : square_at[(g, t)] + S] if (g, t) in square_at else h
+            banks = [first_product(g, t, js) for js in halves]
+            for x, js in zip(banks, halves):
+                nc.scalar.activation(out=sq[:, js], in_=x, func=ACT.Square)
+            for js in halves:
+                nc.scalar.activation(out=h[:, js], in_=sq[:, js], func=ACT.Ln, bias=1.0)
+            if with_gain:
+                apply_gain(g, t, h, h)
+            return h
+
+        def scatter(g, t, h, js, factor=None):
+            nc.vector.tensor_tensor(
+                out=page[g][t][:].indirect(offs2_sb[:, js.start // 16 : js.stop // 16]),
+                in0=h[:, js],
+                in1=(wg[t] if factor is None else factor)[:, js],
+                op=ALU.mult,
+            )
+
+        def store_page(g, t):
+            nc.sync.dma_start(out=page_out[g, t], in_=page[g][t][:])
+
+        pairs = {}
+
+        def pair_cast(g, t, c):
+            if t == 0:
+                pairs[(g, c)] = rotating([P, PACK * BANK], BF16, f"pair{g}{c}", "pair")
+            view = pairs[(g, c)][:].rearrange("p (u m e) -> p u m e", u=2, e=2)
+            nc.scalar.copy(out=view[:, t // 2, :, t % 2], in_=page[g][t][:, BANK * c : BANK * (c + 1)])
+
+        staged = {}
+
+        def weave(g, c, engine):
+            st = rotating([P, PACK * BANK], BF16, f"pst{g}{c}", "stage")
+            if g == 0:
+                words = pair0_words.rearrange("p (u m) -> p m u", u=2)[:, BANK * c : BANK * (c + 1), :]
+            else:
+                words = pairs[(g, c)][:].bitcast(F32).rearrange("p (u m) -> p m u", u=2)
+            copy_on(engine, st[:].bitcast(F32).rearrange("p (m u) -> p m u", u=2), words)
+            staged[(g, c)] = st
+
+        def quantize_page(g, c):
+            cols = slice(BANK * c, BANK * (c + 1))
+            nc.vector.quantize_mx(out=pc[g][:, cols].bitcast(FP8X4), scales=ps[g][:, cols], in_=staged[(g, c)][:])
+
+        def store_codes(g, cols):
+            words = out_2[g].rearrange("p m t -> p (m t)").bitcast(I32)
+            nc.sync.dma_start(out=words[:, cols], in_=pc[g][:, cols].bitcast(I32))
+
+        def store_scales(g):
+            for q in range(QUADS):
+                nc.sync.dma_start(
+                    out=out_3[g, 4 * q : 4 * q + 4, :].bitcast(I32),
+                    in_=ps[g][32 * q : 32 * q + 4, :].bitcast(I32),
+                )
+
+        def stage_one(g, t, h=None):
+            h = make_h(g, t, new_h(g, t) if h is None else h)
+            scatter(g, t, h, slice(0, S))
+            store_page(g, t)
+
+        def pair_all(g, t):
+            if g == 0:
+                view = pair0[:].rearrange("p (u m e) -> p u m e", u=2, e=2)
+                nc.scalar.copy(out=view[:, t // 2, :, t % 2], in_=page[g][t][:])
+            else:
+                for c in range(CHUNKS):
+                    pair_cast(g, t, c)
+
+        h00, h01 = new_h(0, 0), new_h(0, 1)
+        wg00 = rotating([P, S], F32, "wg00", "pair")
+        for js in halves:
+            nc.vector.tensor_scalar(
+                out=wg00[:, js], in0=wg[0][:, js], scalar1=gain_sb[:, 0, 0:1], scalar2=None, op0=ALU.mult
+            )
+        scratch = [h01[:, S // 4 : HALF], h01[:, HALF : 3 * S // 4], h01[:, 0:HALF]]
+        for group in ([0, 1], [2]):
+            for i in group:
+                nc.scalar.activation(out=scratch[i], in_=first_product(0, 0, first_pieces[i]), func=ACT.Square)
+            for i in group:
+                nc.scalar.activation(out=h00[:, first_pieces[i]], in_=scratch[i], func=ACT.Ln, bias=1.0)
+        for js in first_pieces:
+            scatter(0, 0, h00, js, wg00[:])
+        store_page(0, 0)
+        stage_one(0, 1, h01)
+        stage_one(0, 2)
+        cast_w1(1, 0, ["scalar"])
+        cast_w1(1, 1, ["scalar"])
+        stage_one(0, 3)
+        pair_all(0, 0)
+        stage_one(1, 0)
+        pair_all(0, 1)
+        stage_one(1, 1)
+        stage_one(1, 2)
+        pair_all(0, 2)
+        pair_all(0, 3)
+        h_last = make_h(1, 3, new_h(1, 3), with_gain=False)
+
+        wb_st = rotating([P, GROUPS * PACK * N], BF16, "wb_st", "h")
+        for g in range(GROUPS):
+            nc.scalar.copy(
+                out=wb_st[:, g * PACK * N : (g + 1) * PACK * N].rearrange("p (c i j) -> p c j i", i=4, j=PACK),
+                in_=wb_raw[:, g, :].rearrange("p (j c i) -> p c j i", i=4, j=PACK),
+            )
+        for c in range(CHUNKS):
+            weave(0, c, "vector")
+        for c in range(CHUNKS):
+            quantize_page(0, c)
+        store_codes(0, slice(0, T2))
+        store_scales(0)
+        pair_all(1, 0)
+        apply_gain(1, 3, pair0_words[:, 0:S], h_last)
+        scatter(1, 3, pair0_words[:, 0:S], slice(0, S))
+        store_page(1, 3)
+        pair_all(1, 1)
+        pair_all(1, 2)
+        wbc = keep.tile([P, GROUPS * N], U32, name="wbc", tag="wg_rest", align_bytes=64)
+        nc.vector.quantize_mx(out=wbc[:].bitcast(FP8X4), scales=wbs[:], in_=wb_st[:])
+
+        sums = {}
+
+        def product(c, n, g, which=("a", "b")):
+            cols = slice(BANK * c, BANK * (c + 1))
+            if (c, n) not in sums:
+                ya = psum.tile([P, BANK], F32, name=f"ya{c}{n}", tag="bank")
+                yb = psum.tile([P, BANK], F32, name=f"yb{c}{n}", tag="bank")
+                sums[(c, n)] = (ya, yb)
+            ya, yb = sums[(c, n)]
+            if "a" in which:
+                product_a(ya, cols, n, g)
+            if "b" in which:
+                product_b(yb, cols, n, g)
+
+        def product_a(ya, cols, n, g):
+            nc.tensor.matmul_mx(
+                out=ya[:],
+                lhsT=waw[:, g, 2 * P * n : 2 * P * (n + 1)].bitcast(FP4X4),
+                lhsT_scale=was[:, g, P * n : P * (n + 1)],
+                rhs=pc[g][:, cols].bitcast(FP8X4),
+                rhs_scale=ps[g][:, cols],
+                start=(g == 0),
+                stop=(g == GROUPS - 1),
+            )
+
+        def product_b(yb, cols, n, g):
+            wcols = slice(N * g + P * n, N * g + P * (n + 1))
+            nc.tensor.matmul_mx(
+                out=yb[:],
+                lhsT=wbc[:, wcols].bitcast(FP8X4),
+                lhsT_scale=wbs[:, wcols],
+                rhs=pc[g][:, cols].bitcast(FP8X4),
+                rhs_scale=ps[g][:, cols],
+                start=(g == 0),
+                stop=(g == GROUPS - 1),
+            )
+
+        y = [keep.tile([P, T2], F32, name=f"y{n}", tag=f"raw0{n}", align_bytes=64) for n in range(N // P)]
+
+        def finish(c, n):
+            ya, yb = sums[(c, n)]
+            ya_sb = rotating([P, BANK], F32, f"ya_sb{c}{n}", "h")
+            nc.scalar.copy(out=ya_sb[:], in_=ya[:])
+            cols = slice(BANK * c, BANK * (c + 1))
+            nc.vector.tensor_tensor(out=y[n][:, cols], in0=yb[:], in1=ya_sb[:], op=ALU.max)
+            nc.sync.dma_start(out=out_0[P * n : P * (n + 1), cols], in_=y[n][:, cols])
+
+        for which in ("a", "b"):
+            for c in range(2):
+                for n in range(N // P):
+                    product(c, n, 0, which)
+        def close(c):
+            for n in range(N // P):
+                for which in ("a", "b"):
+                    for g in range(GROUPS) if c >= 2 else [1]:
+                        product(c, n, g, which)
+                finish(c, n)
+
+        def planes(c, engine):
+            weave(1, c, engine)
+            quantize_page(1, c)
+            store_codes(1, slice(BANK * c, BANK * (c + 1)))
+
+        for c in range(CHUNKS):
+            pair_cast(1, PACK - 1, c)
+        planes(0, "vector")
+        planes(1, "vector")
+        close(0)
+        planes(2, "vector")
+        planes(3, "scalar")
+        store_scales(1)
+        for c in range(1, CHUNKS):
+            close(c)

@@ -1,6 +1,7 @@
 from contextlib import ExitStack
 
 import concourse.mybir as mybir
+from concourse.masks import make_identity
 
 K, H, N, T, S, T2 = 1024, 1024, 256, 2048, 1024, 2048
 FLOPS = 2 * K * H * S + 2 * 2 * H * N * T2
@@ -35,13 +36,21 @@ def tile_list_cyclist_tile_page_kernel(
     with ExitStack() as ctx:
         keep = ctx.enter_context(tc.tile_pool(name="keep", bufs=1))
         ring = ctx.enter_context(tc.tile_pool(name="ring", bufs=4))
-        psum = ctx.enter_context(tc.psum_pool(name="psum", bufs=8))
+        psum = ctx.enter_context(tc.psum_pool(name="psum", bufs=1))
 
         def held(shape, dtype, name):
             return keep.tile(shape, dtype, name=name, align_bytes=64)
 
         def rotating(shape, dtype, name, tag):
             return ring.tile(shape, dtype, name=name, tag=tag, align_bytes=64)
+
+        banks = [psum.tile([P, BANK], F32, name=f"bank{b}") for b in range(8)]
+        taken = []
+
+        def next_bank():
+            turn = len(taken)
+            taken.append(turn)
+            return banks[turn if turn < 8 else (turn + 2) % 8]
 
         offs_sb = keep.tile([P, S // 16], U16, name="offs_sb")
         offs2_sb = keep.tile([P, S // 16], U16, name="offs2_sb")
@@ -50,9 +59,8 @@ def tile_list_cyclist_tile_page_kernel(
         vw = [held([P, S], U32, f"vw{a}") for a in range(PASSES)]
         vs = held([P, S], U8, "vs")
         gain_sb = held([P, GROUPS, PACK], F32, "gain_sb")
-        wg_first = held([P, S], F32, "wg_first")
-        wg_rest = keep.tile([P, (PACK - 1) * S], F32, name="wg_rest", tag="wg_rest", align_bytes=64)
-        wg = [wg_first[:]] + [wg_rest[:, S * t : S * (t + 1)] for t in range(PACK - 1)]
+        wgs_t = held([P, PACK * S], F32, "wgs_t")
+        ident = held([P, P], F32, "ident")
         page = [[held([P, T2], F32, f"page{g}{t}") for t in range(PACK)] for g in range(GROUPS)]
         w1c = [[held([P, KP], U32, f"w1c{g}{a}") for a in range(PASSES)] for g in range(GROUPS)]
         w1s = [[held([P, KP], U8, f"w1s{g}{a}") for a in range(PASSES)] for g in range(GROUPS)]
@@ -77,7 +85,6 @@ def tile_list_cyclist_tile_page_kernel(
 
         page_in = page0.rearrange("(g p t) c -> g t p c", g=GROUPS, t=PACK)
         page_out = out_1.rearrange("(g p t) c -> g t p c", g=GROUPS, t=PACK)
-        wgs_rows = wgs.rearrange("(m t) j -> m (t j)", t=PACK)
         w1_raw = {}
 
         def load_words(a):
@@ -91,10 +98,6 @@ def tile_list_cyclist_tile_page_kernel(
             nc.sync.dma_start(out=raw[:], in_=rows.rearrange("(p j) c -> p j c", j=PACK))
             w1_raw[(g, a)] = raw
 
-        def load_wgs(tile, cols):
-            for q in (0, 2, 1, 3):
-                nc.sync.dma_start(out=tile[32 * q : 32 * (q + 1), :], in_=wgs_rows[:, cols])
-
         def load_page(g, t):
             nc.sync.dma_start(out=page[g][t][:], in_=page_in[g, t])
 
@@ -103,13 +106,13 @@ def tile_list_cyclist_tile_page_kernel(
         nc.sync.dma_start(out=gain_sb[:], in_=gain.rearrange("(g p t) -> p g t", g=GROUPS, t=PACK))
         nc.sync.dma_start(out=waw[:].bitcast(I32), in_=wa4_words.rearrange("g p c -> p g c").bitcast(I32))
         load_words(0)
+        wgs_sb = rotating([P, S], F32, "wgs_sb", "stage")
+        nc.sync.dma_start(out=wgs_sb[:], in_=wgs)
         load_w1(0, 0)
         load_w1(0, 1)
         load_words(1)
         load_page(0, 0)
-        load_wgs(wg_first, slice(0, S))
         load_page(0, 1)
-        load_wgs(wg_rest, slice(S, PACK * S))
         load_w1(1, 0)
         load_w1(1, 1)
         load_page(0, 2)
@@ -144,10 +147,44 @@ def tile_list_cyclist_tile_page_kernel(
         def gather_words(a, lo, hi):
             nc.vector.tensor_copy(out=vw[a][:, lo:hi], in_=tabw[:, T * a : T * (a + 1)].indirect(offs_sb[:, lo // 16 : hi // 16]))
 
+        make_identity(nc, ident[:])
+        turned = []
+        for b in range(S // BANK):
+            bank = next_bank()
+            for i in range(BANK // P):
+                lo = BANK * b + P * i
+                nc.tensor.transpose(bank[:, P * i : P * (i + 1)], wgs_sb[:, lo : lo + P], ident[:])
+            turned.append(bank)
+
+        def spread_wgs(t):
+            for b, bank in enumerate(turned):
+                lo = S * t + BANK * b
+                rows = bank[:].rearrange("p (i m t) -> p t i m", t=PACK, m=32)[:, t]
+                nc.scalar.copy(
+                    out=wgs_t[:, lo : lo + BANK].rearrange("p (i q m) -> p i q m", q=QUADS, m=32),
+                    in_=rows.unsqueeze(2).to_broadcast([P, BANK // P, QUADS, 32]),
+                )
+
+        def make_factor(g, t, out):
+            for b in range(S // BANK):
+                bank = next_bank()
+                for i in range(BANK // P):
+                    lo = S * t + BANK * b + P * i
+                    nc.tensor.transpose(bank[:, P * i : P * (i + 1)], wgs_t[:, lo : lo + P], ident[:])
+                nc.scalar.activation(
+                    out=out[:, BANK * b : BANK * (b + 1)], in_=bank[:], func=ACT.Copy, scale=gain_sb[:, g, t : t + 1]
+                )
+
+        spread_wgs(0)
         gather_words(0, 0, S)
         nc.vector.tensor_copy(out=vs[:], in_=tabs[:].indirect(offs_sb[:]))
-        cast_w1(0, 0, ["scalar"])
+        factor00 = rotating([P, S], F32, "factor00", "pair")
+        make_factor(0, 0, factor00[:])
+        cast_w1(0, 0, ["vector"])
         cast_w1(0, 1, ["scalar", "vector"])
+        factor01 = rotating([P, S], F32, "factor01", "pair")
+        spread_wgs(1)
+        make_factor(0, 1, factor01[:])
         first_pieces = [slice(0, S // 4), slice(S // 4, HALF), slice(HALF, S)]
         for js in first_pieces:
             gather_words(1, js.start, js.stop)
@@ -155,16 +192,12 @@ def tile_list_cyclist_tile_page_kernel(
         pair0 = keep.tile([P, PACK * T2], BF16, name="pair0", tag="wide", align_bytes=64)
         pair0_words = pair0[:].bitcast(F32)
         h_slot = {(0, 3): "raw11", (1, 1): "raw00", (1, 2): "raw01", (1, 3): "raw10"}
-        square_at = {(0, 3): 0, (1, 2): T2}
+        square_at = {(0, 3): HALF, (1, 2): 2 * S + HALF}
         halves = [slice(0, HALF), slice(HALF, S)]
-
-        def apply_gain(g, t, out, h):
-            for js in halves:
-                nc.scalar.activation(out=out[:, js], in_=h[:, js], func=ACT.Copy, scale=gain_sb[:, g, t : t + 1])
 
         def first_product(g, t, js):
             cols = slice(P * t, P * (t + 1))
-            x = psum.tile([P, BANK], F32, name=f"x{g}{t}{js.start}", tag="bank")
+            x = next_bank()
             x = x[:, 0 : js.stop - js.start]
             for a in range(PASSES):
                 nc.tensor.matmul_mx(
@@ -180,27 +213,25 @@ def tile_list_cyclist_tile_page_kernel(
 
         def new_h(g, t):
             if (g, t) in h_slot:
-                h_tile = keep.tile([P, S], F32, name=f"h{g}{t}", tag=h_slot[(g, t)], align_bytes=64)
-            else:
-                h_tile = rotating([P, S], F32, f"h{g}{t}", "h")
-            return h_tile[:]
+                both = keep.tile([P, 2 * S], F32, name=f"h{g}{t}", tag=h_slot[(g, t)], align_bytes=64)
+                return both[:, 0:S], both[:, S : 2 * S]
+            h_tile = rotating([P, S], F32, f"h{g}{t}", "h")
+            factor = rotating([P, S], F32, f"factor{g}{t}", "pair")
+            return h_tile[:], factor[:]
 
-        def make_h(g, t, h, with_gain=True):
+        def make_h(g, t, h):
             sq = pair0_words[:, square_at[(g, t)] : square_at[(g, t)] + S] if (g, t) in square_at else h
-            banks = [first_product(g, t, js) for js in halves]
-            for x, js in zip(banks, halves):
+            xs = [first_product(g, t, js) for js in halves]
+            for x, js in zip(xs, halves):
                 nc.scalar.activation(out=sq[:, js], in_=x, func=ACT.Square)
             for js in halves:
                 nc.scalar.activation(out=h[:, js], in_=sq[:, js], func=ACT.Ln, bias=1.0)
-            if with_gain:
-                apply_gain(g, t, h, h)
-            return h
 
-        def scatter(g, t, h, js, factor=None):
+        def scatter(g, t, h, factor, js):
             nc.vector.tensor_tensor(
                 out=page[g][t][:].indirect(offs2_sb[:, js.start // 16 : js.stop // 16]),
                 in0=h[:, js],
-                in1=(wg[t] if factor is None else factor)[:, js],
+                in1=factor[:, js],
                 op=ALU.mult,
             )
 
@@ -212,18 +243,25 @@ def tile_list_cyclist_tile_page_kernel(
         def pair_cast(g, t, c):
             if t == 0:
                 pairs[(g, c)] = rotating([P, PACK * BANK], BF16, f"pair{g}{c}", "pair")
-            view = pairs[(g, c)][:].rearrange("p (u m e) -> p u m e", u=2, e=2)
-            nc.scalar.copy(out=view[:, t // 2, :, t % 2], in_=page[g][t][:, BANK * c : BANK * (c + 1)])
+            nc.scalar.copy(
+                out=pairs[(g, c)][:, BANK * t : BANK * (t + 1)], in_=page[g][t][:, BANK * c : BANK * (c + 1)]
+            )
 
         staged = {}
 
-        def weave(g, c, engine):
+        def weave(g, c, vector_cols):
             st = rotating([P, PACK * BANK], BF16, f"pst{g}{c}", "stage")
             if g == 0:
-                words = pair0_words.rearrange("p (u m) -> p m u", u=2)[:, BANK * c : BANK * (c + 1), :]
+                rows = pair0[:].rearrange("p (t m) -> p t m", t=PACK)[:, :, BANK * c : BANK * (c + 1)]
             else:
-                words = pairs[(g, c)][:].bitcast(F32).rearrange("p (u m) -> p m u", u=2)
-            copy_on(engine, st[:].bitcast(F32).rearrange("p (m u) -> p m u", u=2), words)
+                rows = pairs[(g, c)][:].rearrange("p (t m) -> p t m", t=PACK)
+            for engine, lo, hi in (("vector", 0, vector_cols), ("scalar", vector_cols, BANK)):
+                if hi > lo:
+                    copy_on(
+                        engine,
+                        st[:, PACK * lo : PACK * hi].rearrange("p (m i t) -> p m t i", i=4, t=PACK),
+                        rows[:, :, lo:hi].rearrange("p t (m i) -> p m t i", i=4),
+                    )
             staged[(g, c)] = st
 
         def quantize_page(g, c):
@@ -241,25 +279,22 @@ def tile_list_cyclist_tile_page_kernel(
                     in_=ps[g][32 * q : 32 * q + 4, :].bitcast(I32),
                 )
 
-        def stage_one(g, t, h=None):
-            h = make_h(g, t, new_h(g, t) if h is None else h)
-            scatter(g, t, h, slice(0, S))
+        def stage_one(g, t):
+            h, factor = new_h(g, t)
+            make_h(g, t, h)
+            make_factor(g, t, factor)
+            scatter(g, t, h, factor, slice(0, S))
             store_page(g, t)
 
         def pair_all(g, t):
             if g == 0:
-                view = pair0[:].rearrange("p (u m e) -> p u m e", u=2, e=2)
-                nc.scalar.copy(out=view[:, t // 2, :, t % 2], in_=page[g][t][:])
+                nc.scalar.copy(out=pair0[:, T2 * t : T2 * (t + 1)], in_=page[g][t][:])
             else:
                 for c in range(CHUNKS):
                     pair_cast(g, t, c)
 
-        h00, h01 = new_h(0, 0), new_h(0, 1)
-        wg00 = rotating([P, S], F32, "wg00", "pair")
-        for js in halves:
-            nc.vector.tensor_scalar(
-                out=wg00[:, js], in0=wg[0][:, js], scalar1=gain_sb[:, 0, 0:1], scalar2=None, op0=ALU.mult
-            )
+        h00 = rotating([P, S], F32, "h00", "h")
+        h01 = rotating([P, S], F32, "h01", "h")
         scratch = [h01[:, S // 4 : HALF], h01[:, HALF : 3 * S // 4], h01[:, 0:HALF]]
         for group in ([0, 1], [2]):
             for i in group:
@@ -267,52 +302,57 @@ def tile_list_cyclist_tile_page_kernel(
             for i in group:
                 nc.scalar.activation(out=h00[:, first_pieces[i]], in_=scratch[i], func=ACT.Ln, bias=1.0)
         for js in first_pieces:
-            scatter(0, 0, h00, js, wg00[:])
+            scatter(0, 0, h00, factor00, js)
         store_page(0, 0)
-        stage_one(0, 1, h01)
+        make_h(0, 1, h01)
+        scatter(0, 1, h01, factor01, slice(0, S))
+        store_page(0, 1)
+        spread_wgs(2)
+        spread_wgs(3)
         stage_one(0, 2)
         cast_w1(1, 0, ["scalar"])
         cast_w1(1, 1, ["scalar"])
         stage_one(0, 3)
         pair_all(0, 0)
-        stage_one(1, 0)
         pair_all(0, 1)
+        stage_one(1, 0)
         stage_one(1, 1)
         stage_one(1, 2)
         pair_all(0, 2)
         pair_all(0, 3)
-        h_last = make_h(1, 3, new_h(1, 3), with_gain=False)
+        h_last = new_h(1, 3)[0]
+        make_h(1, 3, h_last)
 
+        for c in range(CHUNKS):
+            weave(0, c, BANK if c == 0 else 0)
+        for c in range(CHUNKS):
+            quantize_page(0, c)
+        store_codes(0, slice(0, T2))
+        store_scales(0)
         wb_st = rotating([P, GROUPS * PACK * N], BF16, "wb_st", "h")
         for g in range(GROUPS):
             nc.scalar.copy(
                 out=wb_st[:, g * PACK * N : (g + 1) * PACK * N].rearrange("p (c i j) -> p c j i", i=4, j=PACK),
                 in_=wb_raw[:, g, :].rearrange("p (j c i) -> p c j i", i=4, j=PACK),
             )
-        for c in range(CHUNKS):
-            weave(0, c, "vector")
-        for c in range(CHUNKS):
-            quantize_page(0, c)
-        store_codes(0, slice(0, T2))
-        store_scales(0)
         pair_all(1, 0)
-        apply_gain(1, 3, pair0_words[:, 0:S], h_last)
-        scatter(1, 3, pair0_words[:, 0:S], slice(0, S))
+        make_factor(1, 3, pair0_words[:, 0:S])
+        scatter(1, 3, h_last, pair0_words[:, 0:S], slice(0, S))
         store_page(1, 3)
         pair_all(1, 1)
         pair_all(1, 2)
-        wbc = keep.tile([P, GROUPS * N], U32, name="wbc", tag="wg_rest", align_bytes=64)
+        wbc = keep.tile([P, GROUPS * N], U32, name="wbc", tag="raw10", align_bytes=64)
         nc.vector.quantize_mx(out=wbc[:].bitcast(FP8X4), scales=wbs[:], in_=wb_st[:])
 
         sums = {}
+        banks_a = [next_bank() for i in range(4)]
+        banks_b = [next_bank() for i in range(4)]
+        for i in range(4):
+            sums[(i // 2, i % 2)] = (banks_a[i], banks_b[i])
 
         def product(c, n, g, which=("a", "b")):
             cols = slice(BANK * c, BANK * (c + 1))
-            if (c, n) not in sums:
-                ya = psum.tile([P, BANK], F32, name=f"ya{c}{n}", tag="bank")
-                yb = psum.tile([P, BANK], F32, name=f"yb{c}{n}", tag="bank")
-                sums[(c, n)] = (ya, yb)
-            ya, yb = sums[(c, n)]
+            ya, yb = sums[(c % 2, n)]
             if "a" in which:
                 product_a(ya, cols, n, g)
             if "b" in which:
@@ -344,7 +384,7 @@ def tile_list_cyclist_tile_page_kernel(
         y = [keep.tile([P, T2], F32, name=f"y{n}", tag=f"raw0{n}", align_bytes=64) for n in range(N // P)]
 
         def finish(c, n):
-            ya, yb = sums[(c, n)]
+            ya, yb = sums[(c % 2, n)]
             ya_sb = rotating([P, BANK], F32, f"ya_sb{c}{n}", "h")
             nc.scalar.copy(out=ya_sb[:], in_=ya[:])
             cols = slice(BANK * c, BANK * (c + 1))
@@ -362,18 +402,17 @@ def tile_list_cyclist_tile_page_kernel(
                         product(c, n, g, which)
                 finish(c, n)
 
-        def planes(c, engine):
-            weave(1, c, engine)
+        def planes(c):
+            pair_cast(1, PACK - 1, c)
+            weave(1, c, 320)
             quantize_page(1, c)
             store_codes(1, slice(BANK * c, BANK * (c + 1)))
 
-        for c in range(CHUNKS):
-            pair_cast(1, PACK - 1, c)
-        planes(0, "vector")
-        planes(1, "vector")
+        planes(0)
+        planes(1)
         close(0)
-        planes(2, "vector")
-        planes(3, "scalar")
+        planes(2)
+        planes(3)
         store_scales(1)
         for c in range(1, CHUNKS):
             close(c)

@@ -228,12 +228,8 @@ def tile_list_cyclist_tile_page_kernel(
                 nc.scalar.activation(out=h[:, js], in_=sq[:, js], func=ACT.Ln, bias=1.0)
 
         def scatter(g, t, h, factor, js):
-            nc.vector.tensor_tensor(
-                out=page[g][t][:].indirect(offs2_sb[:, js.start // 16 : js.stop // 16]),
-                in0=h[:, js],
-                in1=factor[:, js],
-                op=ALU.mult,
-            )
+            nc.gpsimd.tensor_tensor(out=h[:, js], in0=h[:, js], in1=factor[:, js], op=ALU.mult)
+            nc.vector.tensor_copy(out=page[g][t][:].indirect(offs2_sb[:, js.start // 16 : js.stop // 16]), in_=h[:, js])
 
         def store_page(g, t):
             nc.sync.dma_start(out=page_out[g, t], in_=page[g][t][:])

@@ -26,6 +26,9 @@ GROUPS = H // KP
 CHUNKS = T2 // BANK
 QUADS = 4
 HALF = S // 2
+RUN = 4
+LAST = 256
+SPLIT = 1152
 
 
 def tile_list_cyclist_tile_page_kernel(
@@ -35,26 +38,23 @@ def tile_list_cyclist_tile_page_kernel(
     nc = tc.nc
     with ExitStack() as ctx:
         keep = ctx.enter_context(tc.tile_pool(name="keep", bufs=1))
-        ring = ctx.enter_context(tc.tile_pool(name="ring", bufs=4))
+        ring = ctx.enter_context(tc.tile_pool(name="ring", bufs=5))
         psum = ctx.enter_context(tc.psum_pool(name="psum", bufs=1))
 
-        def held(shape, dtype, name):
-            return keep.tile(shape, dtype, name=name, align_bytes=64)
+        def held(shape, dtype, name, tag=None):
+            return keep.tile(shape, dtype, name=name, tag=tag or name, align_bytes=64)
 
-        def rotating(shape, dtype, name, tag):
-            return ring.tile(shape, dtype, name=name, tag=tag, align_bytes=64)
+        def staging(name, turn):
+            return held([P, 2 * PACK * BANK], BF16, name, f"stage{turn}")
+
+        def rotating(shape, dtype, name):
+            return ring.tile(shape, dtype, name=name, tag="ring", align_bytes=64)
 
         banks = [psum.tile([P, BANK], F32, name=f"bank{b}") for b in range(8)]
-        taken = []
-
-        def next_bank():
-            turn = len(taken)
-            taken.append(turn)
-            return banks[turn if turn < 8 else (turn + 2) % 8]
 
         offs_sb = keep.tile([P, S // 16], U16, name="offs_sb")
         offs2_sb = keep.tile([P, S // 16], U16, name="offs2_sb")
-        tabw = keep.tile([P, PASSES * T], U32, name="tabw", tag="wide", align_bytes=64)
+        tabw = held([P, PASSES * T], U32, "tabw", "wide")
         tabs = held([P, T], U8, "tabs")
         vw = [held([P, S], U32, f"vw{a}") for a in range(PASSES)]
         vs = held([P, S], U8, "vs")
@@ -62,14 +62,15 @@ def tile_list_cyclist_tile_page_kernel(
         wgs_t = held([P, PACK * S], F32, "wgs_t")
         ident = held([P, P], F32, "ident")
         page = [[held([P, T2], F32, f"page{g}{t}") for t in range(PACK)] for g in range(GROUPS)]
-        w1c = [[held([P, KP], U32, f"w1c{g}{a}") for a in range(PASSES)] for g in range(GROUPS)]
-        w1s = [[held([P, KP], U8, f"w1s{g}{a}") for a in range(PASSES)] for g in range(GROUPS)]
+        w1c = [held([P, PASSES * KP], U32, f"w1c{g}") for g in range(GROUPS)]
+        w1s = [held([P, PASSES * KP], U8, f"w1s{g}") for g in range(GROUPS)]
         pc = [held([P, T2], U32, f"pc{g}") for g in range(GROUPS)]
         ps = [held([P, T2], U8, f"ps{g}") for g in range(GROUPS)]
-        wb_raw = held([P, GROUPS, PACK * N], F32, "wb_raw")
         wbs = held([P, GROUPS * N], U8, "wbs")
         waw = held([P, GROUPS, 2 * N], U8, "waw")
         was = held([P, GROUPS, N], U8, "was")
+        planes = held([P, PACK * T2], BF16, "planes")
+        planes_words = planes[:].bitcast(F32)
         warm = held([P, 2], F32, "warm")
 
         nc.vector.memset(warm[:, 0:1], 1.0)
@@ -93,7 +94,7 @@ def tile_list_cyclist_tile_page_kernel(
             )
 
         def load_w1(g, a):
-            raw = keep.tile([P, PACK, KP], F32, name=f"w1raw{g}{a}", tag=f"raw{g}{a}", align_bytes=64)
+            raw = held([P, PACK, KP], F32, f"w1raw{g}{a}", f"raw{g}{a}")
             rows = w1[KP * a : KP * (a + 1), KP * g : KP * (g + 1)]
             nc.sync.dma_start(out=raw[:], in_=rows.rearrange("(p j) c -> p j c", j=PACK))
             w1_raw[(g, a)] = raw
@@ -106,7 +107,7 @@ def tile_list_cyclist_tile_page_kernel(
         nc.sync.dma_start(out=gain_sb[:], in_=gain.rearrange("(g p t) -> p g t", g=GROUPS, t=PACK))
         nc.sync.dma_start(out=waw[:].bitcast(I32), in_=wa4_words.rearrange("g p c -> p g c").bitcast(I32))
         load_words(0)
-        wgs_sb = rotating([P, S], F32, "wgs_sb", "stage")
+        wgs_sb = rotating([P, S], F32, "wgs_sb")
         nc.sync.dma_start(out=wgs_sb[:], in_=wgs)
         load_w1(0, 0)
         load_w1(0, 1)
@@ -115,9 +116,10 @@ def tile_list_cyclist_tile_page_kernel(
         load_page(0, 1)
         load_w1(1, 0)
         load_w1(1, 1)
+        wb_raw = held([P, GROUPS, PACK * N], F32, "wb_raw")
+        nc.sync.dma_start(out=wb_raw[:], in_=wb.rearrange("(g p j) n -> p g (j n)", g=GROUPS, j=PACK))
         load_page(0, 2)
         load_page(0, 3)
-        nc.sync.dma_start(out=wb_raw[:], in_=wb.rearrange("(g p j) n -> p g (j n)", g=GROUPS, j=PACK))
         for q in range(QUADS):
             nc.sync.dma_start(
                 out=was[32 * q : 32 * q + 4, :, :].bitcast(I32),
@@ -129,45 +131,51 @@ def tile_list_cyclist_tile_page_kernel(
         def copy_on(engine, out, in_):
             if engine == "vector":
                 nc.vector.tensor_copy(out=out, in_=in_)
-            else:
+            elif engine == "scalar":
                 nc.scalar.copy(out=out, in_=in_)
+            else:
+                nc.gpsimd.tensor_scalar(out=out, in0=in_, scalar1=1.0, scalar2=-0.0, op0=ALU.mult, op1=ALU.add)
 
-        def cast_w1(g, a, engines):
-            st = rotating([P, KP * PACK], BF16, f"w1st{g}{a}", "stage")
+        def cast_w1(g, a, st, engines):
+            part = st[:, PACK * KP * a : PACK * KP * (a + 1)]
             share = P // len(engines)
             for i, engine in enumerate(engines):
                 ms = slice(share * i, share * (i + 1))
                 copy_on(
                     engine,
-                    st[:].rearrange("p (t m j) -> p m j t", t=PACK, j=PACK)[:, ms],
+                    part.rearrange("p (t m j) -> p m j t", t=PACK, j=PACK)[:, ms],
                     w1_raw[(g, a)][:].rearrange("p j (m t) -> p m j t", t=PACK)[:, ms],
                 )
-            nc.vector.quantize_mx(out=w1c[g][a][:].bitcast(FP8X4), scales=w1s[g][a][:], in_=st[:])
 
-        def gather_words(a, lo, hi):
-            nc.vector.tensor_copy(out=vw[a][:, lo:hi], in_=tabw[:, T * a : T * (a + 1)].indirect(offs_sb[:, lo // 16 : hi // 16]))
+        def quantize_w1(g, st, lo, hi):
+            cols = slice(KP * lo, KP * hi)
+            nc.vector.quantize_mx(
+                out=w1c[g][:, cols].bitcast(FP8X4), scales=w1s[g][:, cols], in_=st[:, PACK * KP * lo : PACK * KP * hi]
+            )
 
+        def gather_words(a, js):
+            nc.vector.tensor_copy(
+                out=vw[a][:, js], in_=tabw[:, T * a : T * (a + 1)].indirect(offs_sb[:, js.start // 16 : js.stop // 16])
+            )
+
+        halves = [slice(0, HALF), slice(HALF, S)]
         make_identity(nc, ident[:])
-        turned = []
         for b in range(S // BANK):
-            bank = next_bank()
             for i in range(BANK // P):
                 lo = BANK * b + P * i
-                nc.tensor.transpose(bank[:, P * i : P * (i + 1)], wgs_sb[:, lo : lo + P], ident[:])
-            turned.append(bank)
+                nc.tensor.transpose(banks[b][:, P * i : P * (i + 1)], wgs_sb[:, lo : lo + P], ident[:])
 
         def spread_wgs(t):
-            for b, bank in enumerate(turned):
+            for b in range(S // BANK):
                 lo = S * t + BANK * b
-                rows = bank[:].rearrange("p (i m t) -> p t i m", t=PACK, m=32)[:, t]
+                rows = banks[b][:].rearrange("p (i m t) -> p t i m", t=PACK, m=32)[:, t]
                 nc.scalar.copy(
                     out=wgs_t[:, lo : lo + BANK].rearrange("p (i q m) -> p i q m", q=QUADS, m=32),
                     in_=rows.unsqueeze(2).to_broadcast([P, BANK // P, QUADS, 32]),
                 )
 
-        def make_factor(g, t, out):
-            for b in range(S // BANK):
-                bank = next_bank()
+        def make_factor(g, t, out, pair):
+            for b, bank in enumerate(pair):
                 for i in range(BANK // P):
                     lo = S * t + BANK * b + P * i
                     nc.tensor.transpose(bank[:, P * i : P * (i + 1)], wgs_t[:, lo : lo + P], ident[:])
@@ -175,35 +183,14 @@ def tile_list_cyclist_tile_page_kernel(
                     out=out[:, BANK * b : BANK * (b + 1)], in_=bank[:], func=ACT.Copy, scale=gain_sb[:, g, t : t + 1]
                 )
 
-        spread_wgs(0)
-        gather_words(0, 0, S)
-        nc.vector.tensor_copy(out=vs[:], in_=tabs[:].indirect(offs_sb[:]))
-        factor00 = rotating([P, S], F32, "factor00", "pair")
-        make_factor(0, 0, factor00[:])
-        cast_w1(0, 0, ["vector"])
-        cast_w1(0, 1, ["scalar", "vector"])
-        factor01 = rotating([P, S], F32, "factor01", "pair")
-        spread_wgs(1)
-        make_factor(0, 1, factor01[:])
-        first_pieces = [slice(0, S // 4), slice(S // 4, HALF), slice(HALF, S)]
-        for js in first_pieces:
-            gather_words(1, js.start, js.stop)
-
-        pair0 = keep.tile([P, PACK * T2], BF16, name="pair0", tag="wide", align_bytes=64)
-        pair0_words = pair0[:].bitcast(F32)
-        h_slot = {(0, 3): "raw11", (1, 1): "raw00", (1, 2): "raw01", (1, 3): "raw10"}
-        square_at = {(0, 3): HALF, (1, 2): 2 * S + HALF}
-        halves = [slice(0, HALF), slice(HALF, S)]
-
-        def first_product(g, t, js):
-            cols = slice(P * t, P * (t + 1))
-            x = next_bank()
-            x = x[:, 0 : js.stop - js.start]
+        def first_product(g, t, js, bank):
+            x = bank[:, 0 : js.stop - js.start]
             for a in range(PASSES):
+                cols = slice(KP * a + P * t, KP * a + P * (t + 1))
                 nc.tensor.matmul_mx(
                     out=x,
-                    lhsT=w1c[g][a][:, cols].bitcast(FP8X4),
-                    lhsT_scale=w1s[g][a][:, cols],
+                    lhsT=w1c[g][:, cols].bitcast(FP8X4),
+                    lhsT_scale=w1s[g][:, cols],
                     rhs=vw[a][:, js].bitcast(FP8X4),
                     rhs_scale=vs[4 * a : P, js],
                     start=(a == 0),
@@ -211,58 +198,53 @@ def tile_list_cyclist_tile_page_kernel(
                 )
             return x
 
-        def new_h(g, t):
-            if (g, t) in h_slot:
-                both = keep.tile([P, 2 * S], F32, name=f"h{g}{t}", tag=h_slot[(g, t)], align_bytes=64)
-                return both[:, 0:S], both[:, S : 2 * S]
-            h_tile = rotating([P, S], F32, f"h{g}{t}", "h")
-            factor = rotating([P, S], F32, f"factor{g}{t}", "pair")
-            return h_tile[:], factor[:]
+        tiles = [(g, t) for g in range(GROUPS) for t in range(PACK)]
+        hs, factors = {}, {}
 
-        def make_h(g, t, h):
-            sq = pair0_words[:, square_at[(g, t)] : square_at[(g, t)] + S] if (g, t) in square_at else h
-            xs = [first_product(g, t, js) for js in halves]
+        def x_banks(i):
+            return banks[4 + 2 * (i % 2) : 6 + 2 * (i % 2)]
+
+        def make_h(i, h):
+            g, t = tiles[i]
+            xs = [first_product(g, t, js, bank) for bank, js in zip(x_banks(i), halves)]
             for x, js in zip(xs, halves):
-                nc.scalar.activation(out=sq[:, js], in_=x, func=ACT.Square)
+                nc.scalar.activation(out=h[:, js], in_=x, func=ACT.Square)
             for js in halves:
-                nc.scalar.activation(out=h[:, js], in_=sq[:, js], func=ACT.Ln, bias=1.0)
+                nc.scalar.activation(out=h[:, js], in_=h[:, js], func=ACT.Ln, bias=1.0)
+            hs[i] = h
 
-        def scatter(g, t, h, factor, js):
-            nc.gpsimd.tensor_tensor(out=h[:, js], in0=h[:, js], in1=factor[:, js], op=ALU.mult)
-            nc.vector.tensor_copy(out=page[g][t][:].indirect(offs2_sb[:, js.start // 16 : js.stop // 16]), in_=h[:, js])
+        def weigh(out, h, factor_rows):
+            nc.gpsimd.tensor_tensor(out=out, in0=h, in1=factor_rows, op=ALU.mult)
 
-        def store_page(g, t):
+        def scatter(i, js, values):
+            g, t = tiles[i]
+            nc.vector.tensor_copy(out=page[g][t][:].indirect(offs2_sb[:, js.start // 16 : js.stop // 16]), in_=values)
+
+        def store_page(i):
+            g, t = tiles[i]
             nc.sync.dma_start(out=page_out[g, t], in_=page[g][t][:])
 
-        pairs = {}
+        def cast_page(i, pieces):
+            g, t = tiles[i]
+            width = T2 // pieces
+            for c in range(pieces):
+                cols = slice(width * c, width * (c + 1))
+                copy_on("gpsimd", planes[:, T2 * t + cols.start : T2 * t + cols.stop], page[g][t][:, cols])
 
-        def pair_cast(g, t, c):
-            if t == 0:
-                pairs[(g, c)] = rotating([P, PACK * BANK], BF16, f"pair{g}{c}", "pair")
-            nc.scalar.copy(
-                out=pairs[(g, c)][:, BANK * t : BANK * (t + 1)], in_=page[g][t][:, BANK * c : BANK * (c + 1)]
-            )
+        def weave(st, at, c):
+            rows = planes[:].rearrange("p (t m) -> p t m", t=PACK)[:, :, BANK * c : BANK * (c + 1)]
+            out = st[:, PACK * BANK * at : PACK * BANK * (at + 1)].rearrange("p (m i t) -> p m t i", i=RUN, t=PACK)
+            nc.scalar.copy(out=out, in_=rows.rearrange("p t (m i) -> p m t i", i=RUN))
 
-        staged = {}
+        def round_slot(engine, st, i, cols):
+            g, t = tiles[i]
+            copy_on(engine, st[:].rearrange("p (m t) -> p m t", t=PACK)[:, cols, t], page[g][t][:, cols])
 
-        def weave(g, c, vector_cols):
-            st = rotating([P, PACK * BANK], BF16, f"pst{g}{c}", "stage")
-            if g == 0:
-                rows = pair0[:].rearrange("p (t m) -> p t m", t=PACK)[:, :, BANK * c : BANK * (c + 1)]
-            else:
-                rows = pairs[(g, c)][:].rearrange("p (t m) -> p t m", t=PACK)
-            for engine, lo, hi in (("vector", 0, vector_cols), ("scalar", vector_cols, BANK)):
-                if hi > lo:
-                    copy_on(
-                        engine,
-                        st[:, PACK * lo : PACK * hi].rearrange("p (m i t) -> p m t i", i=4, t=PACK),
-                        rows[:, :, lo:hi].rearrange("p t (m i) -> p m t i", i=4),
-                    )
-            staged[(g, c)] = st
+        def chunk(c):
+            return slice(BANK * c, BANK * (c + 1))
 
-        def quantize_page(g, c):
-            cols = slice(BANK * c, BANK * (c + 1))
-            nc.vector.quantize_mx(out=pc[g][:, cols].bitcast(FP8X4), scales=ps[g][:, cols], in_=staged[(g, c)][:])
+        def quantize_page(g, cols, in_):
+            nc.vector.quantize_mx(out=pc[g][:, cols].bitcast(FP8X4), scales=ps[g][:, cols], in_=in_)
 
         def store_codes(g, cols):
             words = out_2[g].rearrange("p m t -> p (m t)").bitcast(I32)
@@ -275,140 +257,180 @@ def tile_list_cyclist_tile_page_kernel(
                     in_=ps[g][32 * q : 32 * q + 4, :].bitcast(I32),
                 )
 
-        def stage_one(g, t):
-            h, factor = new_h(g, t)
-            make_h(g, t, h)
-            make_factor(g, t, factor)
-            scatter(g, t, h, factor, slice(0, S))
-            store_page(g, t)
+        def factor(i, out, pair):
+            factors[i] = out
+            make_factor(*tiles[i], out, pair)
 
-        def pair_all(g, t):
-            if g == 0:
-                nc.scalar.copy(out=pair0[:, T2 * t : T2 * (t + 1)], in_=page[g][t][:])
-            else:
-                for c in range(CHUNKS):
-                    pair_cast(g, t, c)
+        whole = slice(0, S)
 
-        h00 = rotating([P, S], F32, "h00", "h")
-        h01 = rotating([P, S], F32, "h01", "h")
-        scratch = [h01[:, S // 4 : HALF], h01[:, HALF : 3 * S // 4], h01[:, 0:HALF]]
-        for group in ([0, 1], [2]):
-            for i in group:
-                nc.scalar.activation(out=scratch[i], in_=first_product(0, 0, first_pieces[i]), func=ACT.Square)
-            for i in group:
-                nc.scalar.activation(out=h00[:, first_pieces[i]], in_=scratch[i], func=ACT.Ln, bias=1.0)
+        def place(i):
+            weigh(hs[i], hs[i], factors[i])
+            scatter(i, whole, hs[i])
+            store_page(i)
+
+        gather_words(0, whole)
+        nc.vector.tensor_copy(out=vs[:], in_=tabs[:].indirect(offs_sb[:]))
+        early = [rotating([P, S], F32, f"factor{i}") for i in range(2)]
+        spread_wgs(0)
+        factor(0, early[0][:], banks[2:4])
+        st_w = staging("st_w0", 0)
+        cast_w1(0, 0, st_w, ["vector"])
+        quantize_w1(0, st_w, 0, 1)
+        cast_w1(0, 1, st_w, ["scalar", "vector"])
+        quantize_w1(0, st_w, 1, 2)
+        first_pieces = [slice(0, S // 4), slice(S // 4, HALF), slice(HALF, S)]
         for js in first_pieces:
-            scatter(0, 0, h00, factor00, js)
-        store_page(0, 0)
-        make_h(0, 1, h01)
-        scatter(0, 1, h01, factor01, slice(0, S))
-        store_page(0, 1)
-        spread_wgs(2)
-        spread_wgs(3)
-        stage_one(0, 2)
-        cast_w1(1, 0, ["scalar"])
-        cast_w1(1, 1, ["scalar"])
-        stage_one(0, 3)
-        pair_all(0, 0)
-        pair_all(0, 1)
-        stage_one(1, 0)
-        stage_one(1, 1)
-        stage_one(1, 2)
-        pair_all(0, 2)
-        pair_all(0, 3)
-        h_last = new_h(1, 3)[0]
-        make_h(1, 3, h_last)
+            gather_words(1, js)
+        spread_wgs(1)
+        factor(1, early[1][:], banks[2:4])
 
-        for c in range(CHUNKS):
-            weave(0, c, BANK if c == 0 else 0)
-        for c in range(CHUNKS):
-            quantize_page(0, c)
+        h0 = rotating([P, S], F32, "h0")
+        for b, js in enumerate(first_pieces):
+            nc.scalar.activation(out=h0[:, js], in_=first_product(0, 0, js, banks[4 + b]), func=ACT.Square)
+            nc.scalar.activation(out=h0[:, js], in_=h0[:, js], func=ACT.Ln, bias=1.0)
+            weigh(h0[:, js], h0[:, js], factors[0][:, js])
+            scatter(0, js, h0[:, js])
+        store_page(0)
+
+        def lent(slot):
+            return planes_words[:, S * slot : S * (slot + 1)]
+
+        def stream(i, factor_rows, h):
+            factor(i, factor_rows, x_banks(i - 1))
+            make_h(i, h)
+            place(i)
+
+        make_h(1, rotating([P, S], F32, "h1")[:])
+        place(1)
+        spread_wgs(2)
+        factor(2, rotating([P, S], F32, "factor2")[:], x_banks(1))
+        make_h(2, rotating([P, S], F32, "h2")[:])
+        st_w = staging("st_w1", 1)
+        for a in range(PASSES):
+            cast_w1(1, a, st_w, ["scalar"])
+        quantize_w1(1, st_w, 0, PASSES)
+        wb_st = held([P, GROUPS * PACK * N], BF16, "wb_st", "raw00")
+        copy_on(
+            "gpsimd",
+            wb_st[:].rearrange("p (g c j) -> p g c j", g=GROUPS, j=PACK),
+            wb_raw[:].rearrange("p g (j c) -> p g c j", j=PACK),
+        )
+        weighed = held([P, S], F32, "weighed2", "raw11")
+        weigh(weighed[:], hs[2], factors[2])
+        scatter(2, whole, weighed[:])
+        store_page(2)
+        spread_wgs(3)
+        factor(3, planes_words[:, HALF : HALF + S], x_banks(2))
+        factor(4, lent(2), banks[2:4])
+        make_h(3, rotating([P, S], F32, "h3")[:])
+        place(3)
+        cast_page(0, 1)
+        cast_page(1, 1)
+        factor(5, lent(3), banks[0:2])
+        for i in (4, 5):
+            make_h(i, rotating([P, S], F32, f"h{i}")[:])
+            place(i)
+            cast_page(i - 2, 1 if i < 5 else 2)
+        stream(6, held([P, S], F32, "factor6", "wide")[:], held([P, S], F32, "h6", "raw11")[:])
+
+        late = held([P, 2 * S], F32, "late", "raw10")
+        h7 = late[:, S : 2 * S]
+        most, rest = slice(0, S - LAST), slice(S - LAST, S)
+        factor(7, late[:, 0:S], x_banks(6))
+        for bank, js in zip(x_banks(7), halves):
+            nc.scalar.activation(out=h7[:, js], in_=first_product(1, 3, js, bank), func=ACT.Square)
+        nc.scalar.activation(out=h7[:, most], in_=h7[:, most], func=ACT.Ln, bias=1.0)
+        for pair in range(CHUNKS // 2):
+            st = staging(f"st_p{pair}", pair)
+            for at in range(2):
+                weave(st, at, 2 * pair + at)
+            quantize_page(0, slice(2 * BANK * pair, 2 * BANK * (pair + 1)), st[:])
         store_codes(0, slice(0, T2))
         store_scales(0)
-        wb_st = rotating([P, GROUPS * PACK * N], BF16, "wb_st", "h")
-        for g in range(GROUPS):
-            nc.scalar.copy(
-                out=wb_st[:, g * PACK * N : (g + 1) * PACK * N].rearrange("p (c i j) -> p c j i", i=4, j=PACK),
-                in_=wb_raw[:, g, :].rearrange("p (j c i) -> p c j i", i=4, j=PACK),
-            )
-        pair_all(1, 0)
-        make_factor(1, 3, pair0_words[:, 0:S])
-        scatter(1, 3, h_last, pair0_words[:, 0:S], slice(0, S))
-        store_page(1, 3)
-        pair_all(1, 1)
-        pair_all(1, 2)
-        wbc = keep.tile([P, GROUPS * N], U32, name="wbc", tag="raw10", align_bytes=64)
+        st1 = held([P, PACK * T2], BF16, "st1", "wide")
+        for i in (4, 5):
+            round_slot("gpsimd", st1, i, slice(0, SPLIT))
+            round_slot("scalar", st1, i, slice(SPLIT, T2))
+        weighed = lent(0)[:, LAST:S]
+        weigh(weighed, h7[:, most], factors[7][:, most])
+        scatter(7, most, weighed)
+        wbc = held([P, GROUPS * N], U32, "wbc", "planes")
         nc.vector.quantize_mx(out=wbc[:].bitcast(FP8X4), scales=wbs[:], in_=wb_st[:])
+        round_slot("scalar", st1, 6, chunk(0))
+        round_slot("scalar", st1, 6, chunk(2))
+        h_rest = held([P, LAST], F32, "h_rest", "raw11")
+        nc.scalar.activation(out=h_rest[:], in_=h7[:, rest], func=ACT.Ln, bias=1.0)
+        weigh(h_rest[:], h_rest[:], factors[7][:, rest])
+        scatter(7, rest, h_rest[:])
+        round_slot("scalar", st1, 6, chunk(1))
+        round_slot("scalar", st1, 6, chunk(3))
+        store_page(7)
 
-        sums = {}
-        banks_a = [next_bank() for i in range(4)]
-        banks_b = [next_bank() for i in range(4)]
-        for i in range(4):
-            sums[(i // 2, i % 2)] = (banks_a[i], banks_b[i])
-
-        def product(c, n, g, which=("a", "b")):
-            cols = slice(BANK * c, BANK * (c + 1))
-            ya, yb = sums[(c % 2, n)]
-            if "a" in which:
-                product_a(ya, cols, n, g)
-            if "b" in which:
-                product_b(yb, cols, n, g)
-
-        def product_a(ya, cols, n, g):
+        def product(c, n, g, which, lo=0, hi=BANK):
+            cols = slice(BANK * c + lo, BANK * c + hi)
+            bank = banks[4 * (c % 2) + 2 * n + which]
+            if which == 0:
+                lhsT = waw[:, g, 2 * P * n : 2 * P * (n + 1)].bitcast(FP4X4)
+                lhsT_scale = was[:, g, P * n : P * (n + 1)]
+            else:
+                wcols = slice(N * g + P * n, N * g + P * (n + 1))
+                lhsT = wbc[:, wcols].bitcast(FP8X4)
+                lhsT_scale = wbs[:, wcols]
             nc.tensor.matmul_mx(
-                out=ya[:],
-                lhsT=waw[:, g, 2 * P * n : 2 * P * (n + 1)].bitcast(FP4X4),
-                lhsT_scale=was[:, g, P * n : P * (n + 1)],
+                out=bank[:, lo:hi],
+                lhsT=lhsT,
+                lhsT_scale=lhsT_scale,
                 rhs=pc[g][:, cols].bitcast(FP8X4),
                 rhs_scale=ps[g][:, cols],
                 start=(g == 0),
-                stop=(g == GROUPS - 1),
+                stop=(g == GROUPS - 1 and hi == BANK),
             )
 
-        def product_b(yb, cols, n, g):
-            wcols = slice(N * g + P * n, N * g + P * (n + 1))
-            nc.tensor.matmul_mx(
-                out=yb[:],
-                lhsT=wbc[:, wcols].bitcast(FP8X4),
-                lhsT_scale=wbs[:, wcols],
-                rhs=pc[g][:, cols].bitcast(FP8X4),
-                rhs_scale=ps[g][:, cols],
-                start=(g == 0),
-                stop=(g == GROUPS - 1),
-            )
-
-        y = [keep.tile([P, T2], F32, name=f"y{n}", tag=f"raw0{n}", align_bytes=64) for n in range(N // P)]
+        y = [held([P, T2], F32, f"y{n}", f"raw{n}{1 - n}") for n in range(N // P)]
+        ya_sb = held([P, CHUNKS * BANK], F32, "ya_sb", "raw11")
 
         def finish(c, n):
-            ya, yb = sums[(c % 2, n)]
-            ya_sb = rotating([P, BANK], F32, f"ya_sb{c}{n}", "h")
-            nc.scalar.copy(out=ya_sb[:], in_=ya[:])
+            ya, yb = banks[4 * (c % 2) + 2 * n], banks[4 * (c % 2) + 2 * n + 1]
+            at = (2 * c + n) % CHUNKS
+            kept = ya_sb[:, BANK * at : BANK * (at + 1)]
+            nc.scalar.copy(out=kept, in_=ya[:])
             cols = slice(BANK * c, BANK * (c + 1))
-            nc.vector.tensor_tensor(out=y[n][:, cols], in0=yb[:], in1=ya_sb[:], op=ALU.max)
+            nc.vector.tensor_tensor(out=y[n][:, cols], in0=yb[:], in1=kept, op=ALU.max)
             nc.sync.dma_start(out=out_0[P * n : P * (n + 1), cols], in_=y[n][:, cols])
 
-        for which in ("a", "b"):
+        for which in range(2):
             for c in range(2):
                 for n in range(N // P):
                     product(c, n, 0, which)
+
         def close(c):
-            for n in range(N // P):
-                for which in ("a", "b"):
+            for which in range(2):
+                for n in range(N // P):
                     for g in range(GROUPS) if c >= 2 else [1]:
                         product(c, n, g, which)
+            for n in range(N // P):
                 finish(c, n)
 
-        def planes(c):
-            pair_cast(1, PACK - 1, c)
-            weave(1, c, 320)
-            quantize_page(1, c)
-            store_codes(1, slice(BANK * c, BANK * (c + 1)))
+        def last_planes(cols):
+            quantize_page(1, cols, st1[:, PACK * cols.start : PACK * cols.stop])
 
-        planes(0)
-        planes(1)
-        close(0)
-        planes(2)
-        planes(3)
+        starts = [slice(0, BANK // 2), slice(BANK // 2, BANK)]
+        for cols in starts:
+            round_slot("vector", st1, 7, cols)
+        round_slot("scalar", st1, 7, chunk(1))
+        for cols in starts:
+            last_planes(cols)
+            for n in range(N // P):
+                for which in range(2):
+                    product(0, n, 1, which, cols.start, cols.stop)
+        store_codes(1, chunk(0))
+        round_slot("vector", st1, 7, chunk(2))
+        round_slot("scalar", st1, 7, chunk(3))
+        for c in range(1, CHUNKS):
+            last_planes(chunk(c))
+            store_codes(1, chunk(c))
         store_scales(1)
+        for n in range(N // P):
+            finish(0, n)
         for c in range(1, CHUNKS):
             close(c)

@@ -28,7 +28,6 @@ QUADS = 4
 HALF = S // 2
 RUN = 4
 LAST = 256
-SPLIT = 1152
 
 
 def tile_list_cyclist_tile_page_kernel(
@@ -59,7 +58,7 @@ def tile_list_cyclist_tile_page_kernel(
         vw = [held([P, S], U32, f"vw{a}") for a in range(PASSES)]
         vs = held([P, S], U8, "vs")
         gain_sb = held([P, GROUPS, PACK], F32, "gain_sb")
-        wgs_t = held([P, PACK * S], F32, "wgs_t")
+        spread = [held([P, PACK * BANK + P // 2], F32, f"spread{b}") for b in range(S // BANK)]
         ident = held([P, P], F32, "ident")
         page = [[held([P, T2], F32, f"page{g}{t}") for t in range(PACK)] for g in range(GROUPS)]
         w1c = [held([P, PASSES * KP], U32, f"w1c{g}") for g in range(GROUPS)]
@@ -69,8 +68,7 @@ def tile_list_cyclist_tile_page_kernel(
         wbs = held([P, GROUPS * N], U8, "wbs")
         waw = held([P, GROUPS, 2 * N], U8, "waw")
         was = held([P, GROUPS, N], U8, "was")
-        planes = held([P, PACK * T2], BF16, "planes")
-        planes_words = planes[:].bitcast(F32)
+        pairs = [held([P, PACK * T2], BF16, "pairs0")]
         warm = held([P, 2], F32, "warm")
 
         nc.vector.memset(warm[:, 0:1], 1.0)
@@ -82,6 +80,9 @@ def tile_list_cyclist_tile_page_kernel(
                 out=tabs[32 * q : 32 * q + 4 * PASSES, :].bitcast(I32),
                 in_=tab_scales[:, 4 * q : 4 * q + 4, :].bitcast(I32),
             )
+        for rows in spread:
+            nc.vector.memset(rows[:, 0 : PACK * BANK].rearrange("p (i c) -> p i c", c=P)[:, :, 0 : P // 2], 0.0)
+            nc.vector.memset(rows[:, PACK * BANK : PACK * BANK + P // 2], 0.0)
         nc.vector.memset(was[:].rearrange("p g n -> p (g n)").bitcast(I32), 0)
 
         page_in = page0.rearrange("(g p t) c -> g t p c", g=GROUPS, t=PACK)
@@ -106,9 +107,10 @@ def tile_list_cyclist_tile_page_kernel(
         nc.sync.dma_start(offs2_sb[:], offs2)
         nc.sync.dma_start(out=gain_sb[:], in_=gain.rearrange("(g p t) -> p g t", g=GROUPS, t=PACK))
         nc.sync.dma_start(out=waw[:].bitcast(I32), in_=wa4_words.rearrange("g p c -> p g c").bitcast(I32))
-        load_words(0)
         wgs_sb = rotating([P, S], F32, "wgs_sb")
-        nc.sync.dma_start(out=wgs_sb[:], in_=wgs)
+        nc.sync.dma_start(out=wgs_sb[:, 0:HALF], in_=wgs[:, 0:HALF])
+        load_words(0)
+        nc.sync.dma_start(out=wgs_sb[:, HALF:S], in_=wgs[:, HALF:S])
         load_w1(0, 0)
         load_w1(0, 1)
         load_words(1)
@@ -116,7 +118,7 @@ def tile_list_cyclist_tile_page_kernel(
         load_page(0, 1)
         load_w1(1, 0)
         load_w1(1, 1)
-        wb_raw = held([P, GROUPS, PACK * N], F32, "wb_raw")
+        wb_raw = held([P, GROUPS, PACK * N], F32, "wb_raw", "raw01")
         nc.sync.dma_start(out=wb_raw[:], in_=wb.rearrange("(g p j) n -> p g (j n)", g=GROUPS, j=PACK))
         load_page(0, 2)
         load_page(0, 3)
@@ -131,20 +133,18 @@ def tile_list_cyclist_tile_page_kernel(
         def copy_on(engine, out, in_):
             if engine == "vector":
                 nc.vector.tensor_copy(out=out, in_=in_)
-            elif engine == "scalar":
-                nc.scalar.copy(out=out, in_=in_)
             else:
-                nc.gpsimd.tensor_scalar(out=out, in0=in_, scalar1=1.0, scalar2=-0.0, op0=ALU.mult, op1=ALU.add)
+                nc.scalar.copy(out=out, in_=in_)
 
         def cast_w1(g, a, st, engines):
             part = st[:, PACK * KP * a : PACK * KP * (a + 1)]
-            share = P // len(engines)
+            share = PACK // len(engines)
             for i, engine in enumerate(engines):
-                ms = slice(share * i, share * (i + 1))
+                ts = slice(share * i, share * (i + 1))
                 copy_on(
                     engine,
-                    part.rearrange("p (t m j) -> p m j t", t=PACK, j=PACK)[:, ms],
-                    w1_raw[(g, a)][:].rearrange("p j (m t) -> p m j t", t=PACK)[:, ms],
+                    part.rearrange("p (t m j) -> p m j t", t=PACK, j=PACK)[:, :, :, ts],
+                    w1_raw[(g, a)][:].rearrange("p j (m t) -> p m j t", t=PACK)[:, :, :, ts],
                 )
 
         def quantize_w1(g, st, lo, hi):
@@ -165,27 +165,31 @@ def tile_list_cyclist_tile_page_kernel(
                 lo = BANK * b + P * i
                 nc.tensor.transpose(banks[b][:, P * i : P * (i + 1)], wgs_sb[:, lo : lo + P], ident[:])
 
-        def spread_wgs(t):
-            for b in range(S // BANK):
-                lo = S * t + BANK * b
-                rows = banks[b][:].rearrange("p (i m t) -> p t i m", t=PACK, m=32)[:, t]
-                nc.scalar.copy(
-                    out=wgs_t[:, lo : lo + BANK].rearrange("p (i q m) -> p i q m", q=QUADS, m=32),
-                    in_=rows.unsqueeze(2).to_broadcast([P, BANK // P, QUADS, 32]),
-                )
+        def spread_wgs(b):
+            blocks = spread[b][:, P // 2 : PACK * BANK + P // 2].rearrange("p (t i q m) -> p i t q m", t=PACK, q=QUADS, m=32)
+            rows = banks[b][:].rearrange("p (i m t) -> p i t m", t=PACK, m=32)
+            nc.scalar.copy(
+                out=blocks[:, :, :, 0:2, :],
+                in_=rows.unsqueeze(3).to_broadcast([P, BANK // P, PACK, 2, 32]),
+            )
 
-        def make_factor(g, t, out, pair):
+        def turn_back(t, pair):
             for b, bank in enumerate(pair):
                 for i in range(BANK // P):
-                    lo = S * t + BANK * b + P * i
-                    nc.tensor.transpose(bank[:, P * i : P * (i + 1)], wgs_t[:, lo : lo + P], ident[:])
-                nc.scalar.activation(
-                    out=out[:, BANK * b : BANK * (b + 1)], in_=bank[:], func=ACT.Copy, scale=gain_sb[:, g, t : t + 1]
-                )
+                    lo = BANK * t + P * i
+                    for shift in (0, P // 2):
+                        nc.tensor.matmul(
+                            bank[:, P * i : P * (i + 1)],
+                            lhsT=spread[b][:, lo + shift : lo + shift + P],
+                            rhs=ident[:],
+                            is_transpose=True,
+                            start=(shift == 0),
+                            stop=(shift != 0),
+                        )
 
-        def first_product(g, t, js, bank):
+        def first_product(g, t, js, bank, order=(1, 0)):
             x = bank[:, 0 : js.stop - js.start]
-            for a in range(PASSES):
+            for a in order:
                 cols = slice(KP * a + P * t, KP * a + P * (t + 1))
                 nc.tensor.matmul_mx(
                     out=x,
@@ -193,52 +197,47 @@ def tile_list_cyclist_tile_page_kernel(
                     lhsT_scale=w1s[g][:, cols],
                     rhs=vw[a][:, js].bitcast(FP8X4),
                     rhs_scale=vs[4 * a : P, js],
-                    start=(a == 0),
-                    stop=(a == PASSES - 1),
+                    start=(a == order[0]),
+                    stop=(a == order[-1]),
                 )
             return x
 
         tiles = [(g, t) for g in range(GROUPS) for t in range(PACK)]
         hs, factors = {}, {}
 
-        def x_banks(i):
-            return banks[4 + 2 * (i % 2) : 6 + 2 * (i % 2)]
+        duo = [banks[2 * i : 2 * i + 2] for i in range(4)]
 
-        def make_h(i, h):
+        def make_h(i, pair, h, squares=None):
             g, t = tiles[i]
-            xs = [first_product(g, t, js, bank) for bank, js in zip(x_banks(i), halves)]
+            squares = h if squares is None else squares
+            xs = [first_product(g, t, js, bank) for bank, js in zip(pair, halves)]
             for x, js in zip(xs, halves):
-                nc.scalar.activation(out=h[:, js], in_=x, func=ACT.Square)
+                nc.scalar.activation(out=squares[:, js], in_=x, func=ACT.Square)
             for js in halves:
-                nc.scalar.activation(out=h[:, js], in_=h[:, js], func=ACT.Ln, bias=1.0)
+                nc.scalar.activation(out=h[:, js], in_=squares[:, js], func=ACT.Ln, bias=1.0)
             hs[i] = h
-
-        def weigh(out, h, factor_rows):
-            nc.gpsimd.tensor_tensor(out=out, in0=h, in1=factor_rows, op=ALU.mult)
 
         def scatter(i, js, values):
             g, t = tiles[i]
-            nc.vector.tensor_copy(out=page[g][t][:].indirect(offs2_sb[:, js.start // 16 : js.stop // 16]), in_=values)
+            nc.vector.tensor_tensor(
+                out=page[g][t][:].indirect(offs2_sb[:, js.start // 16 : js.stop // 16]),
+                in0=values,
+                in1=factors[i][:, js],
+                op=ALU.mult,
+            )
 
         def store_page(i):
             g, t = tiles[i]
             nc.sync.dma_start(out=page_out[g, t], in_=page[g][t][:])
 
-        def cast_page(i, pieces):
+        def round_pair(engine, i, cols):
             g, t = tiles[i]
-            width = T2 // pieces
-            for c in range(pieces):
-                cols = slice(width * c, width * (c + 1))
-                copy_on("gpsimd", planes[:, T2 * t + cols.start : T2 * t + cols.stop], page[g][t][:, cols])
+            plane = pairs[g][:, 2 * T2 * (t // 2) : 2 * T2 * (t // 2 + 1)].rearrange("p (m e) -> p m e", e=2)
+            copy_on(engine, plane[:, cols, t % 2], page[g][t][:, cols])
 
-        def weave(st, at, c):
-            rows = planes[:].rearrange("p (t m) -> p t m", t=PACK)[:, :, BANK * c : BANK * (c + 1)]
-            out = st[:, PACK * BANK * at : PACK * BANK * (at + 1)].rearrange("p (m i t) -> p m t i", i=RUN, t=PACK)
-            nc.scalar.copy(out=out, in_=rows.rearrange("p t (m i) -> p m t i", i=RUN))
-
-        def round_slot(engine, st, i, cols):
-            g, t = tiles[i]
-            copy_on(engine, st[:].rearrange("p (m t) -> p m t", t=PACK)[:, cols, t], page[g][t][:, cols])
+        def weave(engine, out, g, cols):
+            words = pairs[g][:].bitcast(U32).rearrange("p (u m) -> p m u", u=2)[:, cols, :]
+            copy_on(engine, out.bitcast(U32).rearrange("p (m u) -> p m u", u=2), words)
 
         def chunk(c):
             return slice(BANK * c, BANK * (c + 1))
@@ -258,112 +257,109 @@ def tile_list_cyclist_tile_page_kernel(
                 )
 
         def factor(i, out, pair):
+            g, t = tiles[i]
             factors[i] = out
-            make_factor(*tiles[i], out, pair)
+            for bank, js in zip(pair, halves):
+                nc.scalar.activation(out=out[:, js], in_=bank[:], func=ACT.Copy, scale=gain_sb[:, g, t : t + 1])
 
         whole = slice(0, S)
+        row = slice(0, T2)
 
         def place(i):
-            weigh(hs[i], hs[i], factors[i])
             scatter(i, whole, hs[i])
             store_page(i)
 
-        gather_words(0, whole)
+        def fresh(name):
+            return rotating([P, S], F32, name)[:]
+
         nc.vector.tensor_copy(out=vs[:], in_=tabs[:].indirect(offs_sb[:]))
-        early = [rotating([P, S], F32, f"factor{i}") for i in range(2)]
-        spread_wgs(0)
-        factor(0, early[0][:], banks[2:4])
+        gather_words(0, whole)
+        for b in range(S // BANK):
+            spread_wgs(b)
         st_w = staging("st_w0", 0)
-        cast_w1(0, 0, st_w, ["vector"])
-        quantize_w1(0, st_w, 0, 1)
-        cast_w1(0, 1, st_w, ["scalar", "vector"])
-        quantize_w1(0, st_w, 1, 2)
+        early = held([P, 2 * S], F32, "early")
+        for a in range(PASSES):
+            cast_w1(0, a, st_w, ["scalar" if a == 0 else "vector"])
+            quantize_w1(0, st_w, a, a + 1)
+            turn_back(a, duo[1 - a])
+            factor(a, fresh(f"factor{a}"), duo[1 - a])
+        for a in range(PASSES):
+            factor(PACK + a, early[:, S * a : S * (a + 1)], duo[1 - a])
         first_pieces = [slice(0, S // 4), slice(S // 4, HALF), slice(HALF, S)]
         for js in first_pieces:
             gather_words(1, js)
-        spread_wgs(1)
-        factor(1, early[1][:], banks[2:4])
 
-        h0 = rotating([P, S], F32, "h0")
-        for b, js in enumerate(first_pieces):
-            nc.scalar.activation(out=h0[:, js], in_=first_product(0, 0, js, banks[4 + b]), func=ACT.Square)
-            nc.scalar.activation(out=h0[:, js], in_=h0[:, js], func=ACT.Ln, bias=1.0)
-            weigh(h0[:, js], h0[:, js], factors[0][:, js])
+        h0 = fresh("h0")
+        h1 = fresh("h1")
+        for bank, js in zip(banks[4:7], first_pieces):
+            squares = h1[:, HALF : HALF + js.stop - js.start]
+            nc.scalar.activation(out=squares, in_=first_product(0, 0, js, bank, (0, 1)), func=ACT.Square)
+            nc.scalar.activation(out=h0[:, js], in_=squares, func=ACT.Ln, bias=1.0)
             scatter(0, js, h0[:, js])
         store_page(0)
 
         def lent(slot):
-            return planes_words[:, S * slot : S * (slot + 1)]
+            return pairs[0][:].bitcast(F32)[:, S * slot : S * (slot + 1)]
 
-        def stream(i, factor_rows, h):
-            factor(i, factor_rows, x_banks(i - 1))
-            make_h(i, h)
+        def stream(i, pair, h, squares=None):
+            make_h(i, pair, h, squares)
             place(i)
 
-        make_h(1, rotating([P, S], F32, "h1")[:])
-        place(1)
-        spread_wgs(2)
-        factor(2, rotating([P, S], F32, "factor2")[:], x_banks(1))
-        make_h(2, rotating([P, S], F32, "h2")[:])
+        stream(1, duo[3], h1)
         st_w = staging("st_w1", 1)
         for a in range(PASSES):
             cast_w1(1, a, st_w, ["scalar"])
         quantize_w1(1, st_w, 0, PASSES)
-        wb_st = held([P, GROUPS * PACK * N], BF16, "wb_st", "raw00")
-        copy_on(
-            "gpsimd",
-            wb_st[:].rearrange("p (g c j) -> p g c j", g=GROUPS, j=PACK),
-            wb_raw[:].rearrange("p g (j c) -> p g c j", j=PACK),
-        )
-        weighed = held([P, S], F32, "weighed2", "raw11")
-        weigh(weighed[:], hs[2], factors[2])
-        scatter(2, whole, weighed[:])
-        store_page(2)
-        spread_wgs(3)
-        factor(3, planes_words[:, HALF : HALF + S], x_banks(2))
-        factor(4, lent(2), banks[2:4])
-        make_h(3, rotating([P, S], F32, "h3")[:])
-        place(3)
-        cast_page(0, 1)
-        cast_page(1, 1)
-        factor(5, lent(3), banks[0:2])
-        for i in (4, 5):
-            make_h(i, rotating([P, S], F32, f"h{i}")[:])
-            place(i)
-            cast_page(i - 2, 1 if i < 5 else 2)
-        stream(6, held([P, S], F32, "factor6", "wide")[:], held([P, S], F32, "h6", "raw11")[:])
-
-        late = held([P, 2 * S], F32, "late", "raw10")
-        h7 = late[:, S : 2 * S]
-        most, rest = slice(0, S - LAST), slice(S - LAST, S)
-        factor(7, late[:, 0:S], x_banks(6))
-        for bank, js in zip(x_banks(7), halves):
-            nc.scalar.activation(out=h7[:, js], in_=first_product(1, 3, js, bank), func=ACT.Square)
-        nc.scalar.activation(out=h7[:, most], in_=h7[:, most], func=ACT.Ln, bias=1.0)
+        late = held([P, 2 * S], F32, "late", "raw00")
+        turn_back(2, duo[3])
+        factor(2, fresh("factor2"), duo[3])
+        squares = held([P, S], F32, "squares2", "raw10")
+        stream(2, duo[2], fresh("h2"), squares[:])
+        factor(6, late[:, 0:S], duo[3])
+        turn_back(3, duo[2])
+        factor(3, fresh("factor3"), duo[2])
+        stream(3, duo[3], held([P, S], F32, "h3", "raw10")[:])
+        factor(7, late[:, S : 2 * S], duo[2])
+        round_pair("scalar", 0, row)
+        stream(4, duo[2], fresh("h4"), lent(2))
+        round_pair("scalar", 1, row)
+        stream(5, duo[3], fresh("h5"))
+        round_pair("scalar", 2, row)
+        stream(6, duo[2], held([P, S], F32, "h6", "raw11")[:])
+        round_pair("scalar", 3, row)
         for pair in range(CHUNKS // 2):
             st = staging(f"st_p{pair}", pair)
-            for at in range(2):
-                weave(st, at, 2 * pair + at)
-            quantize_page(0, slice(2 * BANK * pair, 2 * BANK * (pair + 1)), st[:])
+            cols = slice(2 * BANK * pair, 2 * BANK * (pair + 1))
+            weave("scalar", st[:], 0, cols)
+            quantize_page(0, cols, st[:])
         store_codes(0, slice(0, T2))
         store_scales(0)
-        st1 = held([P, PACK * T2], BF16, "st1", "wide")
-        for i in (4, 5):
-            round_slot("gpsimd", st1, i, slice(0, SPLIT))
-            round_slot("scalar", st1, i, slice(SPLIT, T2))
-        weighed = lent(0)[:, LAST:S]
-        weigh(weighed, h7[:, most], factors[7][:, most])
-        scatter(7, most, weighed)
-        wbc = held([P, GROUPS * N], U32, "wbc", "planes")
-        nc.vector.quantize_mx(out=wbc[:].bitcast(FP8X4), scales=wbs[:], in_=wb_st[:])
-        round_slot("scalar", st1, 6, chunk(0))
-        round_slot("scalar", st1, 6, chunk(2))
+
+        h7 = held([P, S], F32, "h7", "spread0")
+        most, rest = slice(0, S - LAST), slice(S - LAST, S)
+        for bank, js in zip(duo[3], halves):
+            nc.scalar.activation(out=h7[:, js], in_=first_product(1, 3, js, bank), func=ACT.Square)
+        h_most = held([P, S - LAST], F32, "h_most", "raw10")
+        nc.scalar.activation(out=h_most[:], in_=h7[:, most], func=ACT.Ln, bias=1.0)
+        scatter(7, most, h_most[:])
+        wb_st = fresh("wb_st").bitcast(BF16)
+        for g in range(GROUPS):
+            nc.scalar.copy(
+                out=wb_st[:, g * PACK * N : (g + 1) * PACK * N].rearrange("p (c i j) -> p c j i", i=RUN, j=PACK),
+                in_=wb_raw[:, g, :].rearrange("p (j c i) -> p c j i", i=RUN, j=PACK),
+            )
+        wbc = held([P, GROUPS * N], U32, "wbc", "raw10")
+        nc.vector.quantize_mx(out=wbc[:].bitcast(FP8X4), scales=wbs[:], in_=wb_st)
+        pairs.append(held([P, PACK * T2], BF16, "pairs1", "wide"))
+        round_pair("scalar", 4, row)
+        round_pair("scalar", 6, chunk(0))
+        round_pair("scalar", 6, chunk(2))
         h_rest = held([P, LAST], F32, "h_rest", "raw11")
         nc.scalar.activation(out=h_rest[:], in_=h7[:, rest], func=ACT.Ln, bias=1.0)
-        weigh(h_rest[:], h_rest[:], factors[7][:, rest])
         scatter(7, rest, h_rest[:])
-        round_slot("scalar", st1, 6, chunk(1))
-        round_slot("scalar", st1, 6, chunk(3))
+        round_pair("scalar", 5, row)
+        round_pair("scalar", 6, chunk(1))
+        round_pair("scalar", 6, chunk(3))
         store_page(7)
 
         def product(c, n, g, which, lo=0, hi=BANK):
@@ -386,7 +382,7 @@ def tile_list_cyclist_tile_page_kernel(
                 stop=(g == GROUPS - 1 and hi == BANK),
             )
 
-        y = [held([P, T2], F32, f"y{n}", f"raw{n}{1 - n}") for n in range(N // P)]
+        y = [held([P, T2], F32, f"y{n}", f"raw0{n}") for n in range(N // P)]
         ya_sb = held([P, CHUNKS * BANK], F32, "ya_sb", "raw11")
 
         def finish(c, n):
@@ -411,26 +407,41 @@ def tile_list_cyclist_tile_page_kernel(
             for n in range(N // P):
                 finish(c, n)
 
-        def last_planes(cols):
-            quantize_page(1, cols, st1[:, PACK * cols.start : PACK * cols.stop])
+        staged = [staging(f"st_last{pair}", pair) for pair in range(CHUNKS // 2)]
 
-        starts = [slice(0, BANK // 2), slice(BANK // 2, BANK)]
-        for cols in starts:
-            round_slot("vector", st1, 7, cols)
-        round_slot("scalar", st1, 7, chunk(1))
-        for cols in starts:
+        def last_stage(cols):
+            at = cols.start % (2 * BANK)
+            return staged[cols.start // (2 * BANK)][:, PACK * at : PACK * (at + cols.stop - cols.start)]
+
+        def last_planes(cols):
+            quantize_page(1, cols, last_stage(cols))
+
+        def halved(c):
+            return [slice(BANK * c, BANK * c + BANK // 2), slice(BANK * c + BANK // 2, BANK * (c + 1))]
+
+        for engine, c in (("vector", 0), ("scalar", 1)):
+            for cols in halved(c):
+                round_pair(engine, 7, cols)
+            for cols in halved(c):
+                weave(engine, last_stage(cols), 1, cols)
+        for cols in halved(0):
             last_planes(cols)
-            for n in range(N // P):
-                for which in range(2):
+            for which in range(2):
+                for n in range(N // P):
                     product(0, n, 1, which, cols.start, cols.stop)
         store_codes(1, chunk(0))
-        round_slot("vector", st1, 7, chunk(2))
-        round_slot("scalar", st1, 7, chunk(3))
-        for c in range(1, CHUNKS):
-            last_planes(chunk(c))
-            store_codes(1, chunk(c))
+        round_pair("vector", 7, chunk(2))
+        last_planes(chunk(1))
+        store_codes(1, chunk(1))
+        round_pair("scalar", 7, chunk(3))
+        weave("vector", last_stage(chunk(2)), 1, chunk(2))
+        finish(0, 0)
+        last_planes(chunk(2))
+        store_codes(1, chunk(2))
+        finish(0, 1)
+        weave("scalar", last_stage(chunk(3)), 1, chunk(3))
+        last_planes(chunk(3))
+        store_codes(1, chunk(3))
         store_scales(1)
-        for n in range(N // P):
-            finish(0, n)
         for c in range(1, CHUNKS):
             close(c)

@@ -37,7 +37,6 @@ def tile_list_cyclist_tile_page_kernel(
     nc = tc.nc
     with ExitStack() as ctx:
         keep = ctx.enter_context(tc.tile_pool(name="keep", bufs=1))
-        ring = ctx.enter_context(tc.tile_pool(name="ring", bufs=5))
         psum = ctx.enter_context(tc.psum_pool(name="psum", bufs=1))
 
         def held(shape, dtype, name, tag=None):
@@ -46,9 +45,6 @@ def tile_list_cyclist_tile_page_kernel(
         def staging(name, turn):
             return held([P, 2 * PACK * BANK], BF16, name, f"stage{turn}")
 
-        def rotating(shape, dtype, name):
-            return ring.tile(shape, dtype, name=name, tag="ring", align_bytes=64)
-
         banks = [psum.tile([P, BANK], F32, name=f"bank{b}") for b in range(8)]
 
         offs_sb = keep.tile([P, S // 16], U16, name="offs_sb")
@@ -56,6 +52,7 @@ def tile_list_cyclist_tile_page_kernel(
         tabw = held([P, PASSES * T], U32, "tabw", "wide")
         tabs = held([P, T], U8, "tabs")
         vw = [held([P, S], U32, f"vw{a}") for a in range(PASSES)]
+        picked = held([P, S], U8, "picked")
         vs = held([P, S], U8, "vs")
         gain_sb = held([P, GROUPS, PACK], F32, "gain_sb")
         spread = [held([P, PACK * BANK + P // 2], F32, f"spread{b}") for b in range(S // BANK)]
@@ -71,19 +68,16 @@ def tile_list_cyclist_tile_page_kernel(
         pairs = [held([P, PACK * T2], BF16, "pairs0")]
         warm = held([P, 2], F32, "warm")
 
+        nc.vector.memset(tabs[32:64, :].bitcast(I32), 0)
+        nc.vector.memset(tabs[64:P, :].bitcast(I32), 0)
         nc.vector.memset(warm[:, 0:1], 1.0)
         nc.scalar.activation(out=warm[:, 1:2], in_=warm[:, 0:1], func=ACT.Ln)
-
-        nc.vector.memset(tabs[:].bitcast(I32), 0)
-        for q in range(QUADS):
-            nc.scalar.dma_start(
-                out=tabs[32 * q : 32 * q + 4 * PASSES, :].bitcast(I32),
-                in_=tab_scales[:, 4 * q : 4 * q + 4, :].bitcast(I32),
-            )
+        make_identity(nc, ident[:])
+        nc.gpsimd.memset(vs[:].bitcast(I32), 0)
         for rows in spread:
-            nc.vector.memset(rows[:, 0 : PACK * BANK].rearrange("p (i c) -> p i c", c=P)[:, :, 0 : P // 2], 0.0)
-            nc.vector.memset(rows[:, PACK * BANK : PACK * BANK + P // 2], 0.0)
-        nc.vector.memset(was[:].rearrange("p g n -> p (g n)").bitcast(I32), 0)
+            nc.gpsimd.memset(rows[:, 0 : PACK * BANK].rearrange("p (i c) -> p i c", c=P)[:, :, 0 : P // 2], 0.0)
+            nc.gpsimd.memset(rows[:, PACK * BANK : PACK * BANK + P // 2], 0.0)
+        nc.gpsimd.memset(was[:].rearrange("p g n -> p (g n)").bitcast(I32), 0)
 
         page_in = page0.rearrange("(g p t) c -> g t p c", g=GROUPS, t=PACK)
         page_out = out_1.rearrange("(g p t) c -> g t p c", g=GROUPS, t=PACK)
@@ -94,34 +88,42 @@ def tile_list_cyclist_tile_page_kernel(
                 out=tabw[:, T * a : T * (a + 1)].bitcast(I32), in_=tab_words[a].rearrange("p n i -> p (n i)").bitcast(I32)
             )
 
-        def load_w1(g, a):
+        def load_w1(g, a, pieces=1):
             raw = held([P, PACK, KP], F32, f"w1raw{g}{a}", f"raw{g}{a}")
-            rows = w1[KP * a : KP * (a + 1), KP * g : KP * (g + 1)]
-            nc.sync.dma_start(out=raw[:], in_=rows.rearrange("(p j) c -> p j c", j=PACK))
+            rows = w1[KP * a : KP * (a + 1), KP * g : KP * (g + 1)].rearrange("(p j) c -> p j c", j=PACK)
+            for i in range(pieces):
+                slots = slice(PACK // pieces * i, PACK // pieces * (i + 1))
+                nc.sync.dma_start(out=raw[:, slots, :], in_=rows[:, slots, :])
             w1_raw[(g, a)] = raw
 
         def load_page(g, t):
             nc.sync.dma_start(out=page[g][t][:], in_=page_in[g, t])
 
         nc.sync.dma_start(offs_sb[:], offs)
-        nc.sync.dma_start(offs2_sb[:], offs2)
-        nc.sync.dma_start(out=gain_sb[:], in_=gain.rearrange("(g p t) -> p g t", g=GROUPS, t=PACK))
-        nc.sync.dma_start(out=waw[:].bitcast(I32), in_=wa4_words.rearrange("g p c -> p g c").bitcast(I32))
-        wgs_sb = rotating([P, S], F32, "wgs_sb")
+        for a in range(PASSES):
+            nc.sync.dma_start(
+                out=tabs[16 * a : 16 * (a + 1), :].bitcast(I32),
+                in_=tab_scales[a].rearrange("(q r) c -> r q c", q=QUADS).bitcast(I32),
+            )
+        wgs_sb = held([P, S], F32, "wgs_sb", "row0")
         nc.sync.dma_start(out=wgs_sb[:, 0:HALF], in_=wgs[:, 0:HALF])
         load_words(0)
         nc.sync.dma_start(out=wgs_sb[:, HALF:S], in_=wgs[:, HALF:S])
-        load_w1(0, 0)
-        load_w1(0, 1)
+        nc.sync.dma_start(out=gain_sb[:], in_=gain.rearrange("(g p t) -> p g t", g=GROUPS, t=PACK))
+        nc.sync.dma_start(offs2_sb[:], offs2)
+        load_w1(0, 0, 2)
+        load_w1(0, 1, 2)
+        nc.vector.tensor_copy(out=picked[:], in_=tabs[:].indirect(offs_sb[:]))
+        for q in range(QUADS):
+            nc.sync.dma_start(out=vs[32 * q : 32 * q + 8, :].bitcast(I32), in_=picked[q:32:QUADS, :].bitcast(I32))
         load_words(1)
         load_page(0, 0)
         load_page(0, 1)
         load_w1(1, 0)
         load_w1(1, 1)
-        wb_raw = held([P, GROUPS, PACK * N], F32, "wb_raw", "raw01")
-        nc.sync.dma_start(out=wb_raw[:], in_=wb.rearrange("(g p j) n -> p g (j n)", g=GROUPS, j=PACK))
         load_page(0, 2)
         load_page(0, 3)
+        nc.sync.dma_start(out=waw[:].bitcast(I32), in_=wa4_words.rearrange("g p c -> p g c").bitcast(I32))
         for q in range(QUADS):
             nc.sync.dma_start(
                 out=was[32 * q : 32 * q + 4, :, :].bitcast(I32),
@@ -129,6 +131,8 @@ def tile_list_cyclist_tile_page_kernel(
             )
         for t in range(PACK):
             load_page(1, t)
+        wb_raw = held([P, GROUPS, PACK * N], F32, "wb_raw", "raw01")
+        nc.sync.dma_start(out=wb_raw[:], in_=wb.rearrange("(g p j) n -> p g (j n)", g=GROUPS, j=PACK))
 
         def copy_on(engine, out, in_):
             if engine == "vector":
@@ -159,7 +163,6 @@ def tile_list_cyclist_tile_page_kernel(
             )
 
         halves = [slice(0, HALF), slice(HALF, S)]
-        make_identity(nc, ident[:])
         for b in range(S // BANK):
             for i in range(BANK // P):
                 lo = BANK * b + P * i
@@ -230,13 +233,20 @@ def tile_list_cyclist_tile_page_kernel(
             g, t = tiles[i]
             nc.sync.dma_start(out=page_out[g, t], in_=page[g][t][:])
 
+        def pair_planes(g, cols):
+            width = T2 if g == 0 else BANK
+            c, at = divmod(cols.start, width)
+            return pairs[g][:, PACK * width * c : PACK * width * (c + 1)], slice(at, at + cols.stop - cols.start)
+
         def round_pair(engine, i, cols):
             g, t = tiles[i]
-            plane = pairs[g][:, 2 * T2 * (t // 2) : 2 * T2 * (t // 2 + 1)].rearrange("p (m e) -> p m e", e=2)
-            copy_on(engine, plane[:, cols, t % 2], page[g][t][:, cols])
+            planes, part = pair_planes(g, cols)
+            out = planes.rearrange("p (u m e) -> p u m e", u=2, e=2)[:, t // 2, part, t % 2]
+            copy_on(engine, out, page[g][t][:, cols])
 
         def weave(engine, out, g, cols):
-            words = pairs[g][:].bitcast(U32).rearrange("p (u m) -> p m u", u=2)[:, cols, :]
+            planes, part = pair_planes(g, cols)
+            words = planes.bitcast(U32).rearrange("p (u m) -> p m u", u=2)[:, part, :]
             copy_on(engine, out.bitcast(U32).rearrange("p (m u) -> p m u", u=2), words)
 
         def chunk(c):
@@ -269,32 +279,34 @@ def tile_list_cyclist_tile_page_kernel(
             scatter(i, whole, hs[i])
             store_page(i)
 
-        def fresh(name):
-            return rotating([P, S], F32, name)[:]
+        def fresh(name, tag):
+            return held([P, S], F32, name, tag)[:]
 
-        nc.vector.tensor_copy(out=vs[:], in_=tabs[:].indirect(offs_sb[:]))
         gather_words(0, whole)
         for b in range(S // BANK):
             spread_wgs(b)
         st_w = staging("st_w0", 0)
-        early = held([P, 2 * S], F32, "early")
         for a in range(PASSES):
-            cast_w1(0, a, st_w, ["scalar" if a == 0 else "vector"])
+            cast_w1(0, a, st_w, ["vector"])
             quantize_w1(0, st_w, a, a + 1)
-            turn_back(a, duo[1 - a])
-            factor(a, fresh(f"factor{a}"), duo[1 - a])
-        for a in range(PASSES):
-            factor(PACK + a, early[:, S * a : S * (a + 1)], duo[1 - a])
+        early = held([P, 2 * S], F32, "early")
+        late = held([P, 2 * S], F32, "late", "raw00")
+        for t, pair, tag in ((0, duo[1], "row1"), (1, duo[0], "row2"), (2, duo[3], "row0")):
+            turn_back(t, pair)
+            factor(t, fresh(f"factor{t}", tag), pair)
+        factor(4, early[:, 0:S], duo[1])
         first_pieces = [slice(0, S // 4), slice(S // 4, HALF), slice(HALF, S)]
         for js in first_pieces:
             gather_words(1, js)
 
-        h0 = fresh("h0")
-        h1 = fresh("h1")
-        for bank, js in zip(banks[4:7], first_pieces):
-            squares = h1[:, HALF : HALF + js.stop - js.start]
-            nc.scalar.activation(out=squares, in_=first_product(0, 0, js, bank, (0, 1)), func=ACT.Square)
-            nc.scalar.activation(out=h0[:, js], in_=squares, func=ACT.Ln, bias=1.0)
+        h0 = fresh("h0", "row3")
+        h1 = fresh("h1", "row4")
+        for bank, js in zip((banks[4], banks[3], banks[2]), first_pieces):
+            runs = (js.stop - js.start) // LAST
+            squares = late[:, HALF : 2 * S].rearrange("p (r c) -> p r c", r=2)[:, 0:runs, 0:LAST]
+            x = first_product(0, 0, js, bank, (0, 1))
+            nc.scalar.activation(out=squares, in_=x.rearrange("p (r c) -> p r c", r=runs), func=ACT.Square)
+            nc.scalar.activation(out=h0[:, js].rearrange("p (r c) -> p r c", r=runs), in_=squares, func=ACT.Ln, bias=1.0)
             scatter(0, js, h0[:, js])
         store_page(0)
 
@@ -305,27 +317,24 @@ def tile_list_cyclist_tile_page_kernel(
             make_h(i, pair, h, squares)
             place(i)
 
-        stream(1, duo[3], h1)
+        stream(1, duo[1], h1)
+        factor(5, late[:, 0:S], duo[0])
+        factor(6, late[:, S : 2 * S], duo[3])
         st_w = staging("st_w1", 1)
-        for a in range(PASSES):
-            cast_w1(1, a, st_w, ["scalar"])
+        cast_w1(1, 0, st_w, ["scalar"])
+        stream(2, duo[2], fresh("h2", "row1"))
+        turn_back(3, duo[1])
+        factor(3, fresh("factor3", "row3"), duo[1])
+        factor(7, early[:, S : 2 * S], duo[1])
+        cast_w1(1, 1, st_w, ["scalar"])
         quantize_w1(1, st_w, 0, PASSES)
-        late = held([P, 2 * S], F32, "late", "raw00")
-        turn_back(2, duo[3])
-        factor(2, fresh("factor2"), duo[3])
-        squares = held([P, S], F32, "squares2", "raw10")
-        stream(2, duo[2], fresh("h2"), squares[:])
-        factor(6, late[:, 0:S], duo[3])
-        turn_back(3, duo[2])
-        factor(3, fresh("factor3"), duo[2])
-        stream(3, duo[3], held([P, S], F32, "h3", "raw10")[:])
-        factor(7, late[:, S : 2 * S], duo[2])
+        stream(3, duo[2], held([P, S], F32, "h3", "raw10")[:])
         round_pair("scalar", 0, row)
-        stream(4, duo[2], fresh("h4"), lent(2))
         round_pair("scalar", 1, row)
-        stream(5, duo[3], fresh("h5"))
+        stream(4, duo[1], fresh("h4", "row2"), lent(2))
+        stream(5, duo[2], fresh("h5", "row4"))
         round_pair("scalar", 2, row)
-        stream(6, duo[2], held([P, S], F32, "h6", "raw11")[:])
+        stream(6, duo[1], held([P, S], F32, "h6", "raw11")[:])
         round_pair("scalar", 3, row)
         for pair in range(CHUNKS // 2):
             st = staging(f"st_p{pair}", pair)
@@ -337,12 +346,12 @@ def tile_list_cyclist_tile_page_kernel(
 
         h7 = held([P, S], F32, "h7", "spread0")
         most, rest = slice(0, S - LAST), slice(S - LAST, S)
-        for bank, js in zip(duo[3], halves):
+        for bank, js in zip(duo[2], halves):
             nc.scalar.activation(out=h7[:, js], in_=first_product(1, 3, js, bank), func=ACT.Square)
         h_most = held([P, S - LAST], F32, "h_most", "raw10")
         nc.scalar.activation(out=h_most[:], in_=h7[:, most], func=ACT.Ln, bias=1.0)
         scatter(7, most, h_most[:])
-        wb_st = fresh("wb_st").bitcast(BF16)
+        wb_st = fresh("wb_st", "row0").bitcast(BF16)
         for g in range(GROUPS):
             nc.scalar.copy(
                 out=wb_st[:, g * PACK * N : (g + 1) * PACK * N].rearrange("p (c i j) -> p c j i", i=RUN, j=PACK),
@@ -351,15 +360,16 @@ def tile_list_cyclist_tile_page_kernel(
         wbc = held([P, GROUPS * N], U32, "wbc", "raw10")
         nc.vector.quantize_mx(out=wbc[:].bitcast(FP8X4), scales=wbs[:], in_=wb_st)
         pairs.append(held([P, PACK * T2], BF16, "pairs1", "wide"))
-        round_pair("scalar", 4, row)
-        round_pair("scalar", 6, chunk(0))
-        round_pair("scalar", 6, chunk(2))
+        for c in range(CHUNKS):
+            round_pair("scalar", 4, chunk(c))
+        for i in (5, 6):
+            for c in range(CHUNKS - 1):
+                round_pair("scalar", i, chunk(c))
         h_rest = held([P, LAST], F32, "h_rest", "raw11")
         nc.scalar.activation(out=h_rest[:], in_=h7[:, rest], func=ACT.Ln, bias=1.0)
         scatter(7, rest, h_rest[:])
-        round_pair("scalar", 5, row)
-        round_pair("scalar", 6, chunk(1))
-        round_pair("scalar", 6, chunk(3))
+        for i in (5, 6):
+            round_pair("scalar", i, chunk(CHUNKS - 1))
         store_page(7)
 
         def product(c, n, g, which, lo=0, hi=BANK):

@@ -107,9 +107,9 @@ def tile_list_cyclist_tile_page_kernel(
             )
         wgs_sb = held([P, S], F32, "wgs_sb", "row0")
         nc.sync.dma_start(out=wgs_sb[:, 0:HALF], in_=wgs[:, 0:HALF])
-        load_words(0)
         nc.sync.dma_start(out=wgs_sb[:, HALF:S], in_=wgs[:, HALF:S])
         nc.sync.dma_start(out=gain_sb[:], in_=gain.rearrange("(g p t) -> p g t", g=GROUPS, t=PACK))
+        load_words(0)
         nc.sync.dma_start(offs2_sb[:], offs2)
         load_w1(0, 0, 2)
         load_w1(0, 1, 2)
@@ -168,12 +168,12 @@ def tile_list_cyclist_tile_page_kernel(
                 lo = BANK * b + P * i
                 nc.tensor.transpose(banks[b][:, P * i : P * (i + 1)], wgs_sb[:, lo : lo + P], ident[:])
 
-        def spread_wgs(b):
+        def spread_wgs(b, ts):
             blocks = spread[b][:, P // 2 : PACK * BANK + P // 2].rearrange("p (t i q m) -> p i t q m", t=PACK, q=QUADS, m=32)
             rows = banks[b][:].rearrange("p (i m t) -> p i t m", t=PACK, m=32)
             nc.scalar.copy(
-                out=blocks[:, :, :, 0:2, :],
-                in_=rows.unsqueeze(3).to_broadcast([P, BANK // P, PACK, 2, 32]),
+                out=blocks[:, :, ts, 0:2, :],
+                in_=rows[:, :, ts].unsqueeze(3).to_broadcast([P, BANK // P, ts.stop - ts.start, 2, 32]),
             )
 
         def turn_back(t, pair):
@@ -283,58 +283,56 @@ def tile_list_cyclist_tile_page_kernel(
             return held([P, S], F32, name, tag)[:]
 
         gather_words(0, whole)
-        for b in range(S // BANK):
-            spread_wgs(b)
+        for ts in (slice(0, 1), slice(1, PACK)):
+            for b in range(S // BANK):
+                spread_wgs(b, ts)
         st_w = staging("st_w0", 0)
         for a in range(PASSES):
             cast_w1(0, a, st_w, ["vector"])
             quantize_w1(0, st_w, a, a + 1)
         early = held([P, 2 * S], F32, "early")
         late = held([P, 2 * S], F32, "late", "raw00")
+        second = (early[:, 0:S], late[:, 0:S], late[:, S : 2 * S])
         for t, pair, tag in ((0, duo[1], "row1"), (1, duo[0], "row2"), (2, duo[3], "row0")):
             turn_back(t, pair)
             factor(t, fresh(f"factor{t}", tag), pair)
-        factor(4, early[:, 0:S], duo[1])
+            factor(PACK + t, second[t], pair)
         first_pieces = [slice(0, S // 4), slice(S // 4, HALF), slice(HALF, S)]
         for js in first_pieces:
             gather_words(1, js)
 
-        h0 = fresh("h0", "row3")
-        h1 = fresh("h1", "row4")
-        for bank, js in zip((banks[4], banks[3], banks[2]), first_pieces):
-            runs = (js.stop - js.start) // LAST
-            squares = late[:, HALF : 2 * S].rearrange("p (r c) -> p r c", r=2)[:, 0:runs, 0:LAST]
-            x = first_product(0, 0, js, bank, (0, 1))
-            nc.scalar.activation(out=squares, in_=x.rearrange("p (r c) -> p r c", r=runs), func=ACT.Square)
-            nc.scalar.activation(out=h0[:, js].rearrange("p (r c) -> p r c", r=runs), in_=squares, func=ACT.Ln, bias=1.0)
-            scatter(0, js, h0[:, js])
-        store_page(0)
-
         def lent(slot):
             return pairs[0][:].bitcast(F32)[:, S * slot : S * (slot + 1)]
+
+        h0 = fresh("h0", "row3")
+        for bank, js in zip((banks[4], banks[3], banks[2]), first_pieces):
+            squares = lent(0)[:, S // 4 : S // 4 + js.stop - js.start]
+            nc.scalar.activation(out=squares, in_=first_product(0, 0, js, bank, (0, 1)), func=ACT.Square)
+            nc.scalar.activation(out=h0[:, js], in_=squares, func=ACT.Ln, bias=1.0)
+            scatter(0, js, h0[:, js])
+        store_page(0)
 
         def stream(i, pair, h, squares=None):
             make_h(i, pair, h, squares)
             place(i)
 
-        stream(1, duo[1], h1)
-        factor(5, late[:, 0:S], duo[0])
-        factor(6, late[:, S : 2 * S], duo[3])
+        odd, even = (banks[5], banks[4]), (banks[3], banks[2])
+        stream(1, odd, fresh("h1", "row4"), lent(0))
         st_w = staging("st_w1", 1)
         cast_w1(1, 0, st_w, ["scalar"])
-        stream(2, duo[2], fresh("h2", "row1"))
-        turn_back(3, duo[1])
-        factor(3, fresh("factor3", "row3"), duo[1])
-        factor(7, early[:, S : 2 * S], duo[1])
+        stream(2, even, fresh("h2", "row1"), lent(0))
+        turn_back(3, odd)
+        factor(3, fresh("factor3", "row3"), odd)
+        factor(7, early[:, S : 2 * S], odd)
         cast_w1(1, 1, st_w, ["scalar"])
         quantize_w1(1, st_w, 0, PASSES)
-        stream(3, duo[2], held([P, S], F32, "h3", "raw10")[:])
+        stream(3, even, held([P, S], F32, "h3", "raw10")[:])
         round_pair("scalar", 0, row)
         round_pair("scalar", 1, row)
-        stream(4, duo[1], fresh("h4", "row2"), lent(2))
-        stream(5, duo[2], fresh("h5", "row4"))
+        stream(4, odd, fresh("h4", "row2"), lent(2))
+        stream(5, even, fresh("h5", "row4"))
         round_pair("scalar", 2, row)
-        stream(6, duo[1], held([P, S], F32, "h6", "raw11")[:])
+        stream(6, odd, held([P, S], F32, "h6", "raw11")[:])
         round_pair("scalar", 3, row)
         for pair in range(CHUNKS // 2):
             st = staging(f"st_p{pair}", pair)
@@ -346,7 +344,7 @@ def tile_list_cyclist_tile_page_kernel(
 
         h7 = held([P, S], F32, "h7", "spread0")
         most, rest = slice(0, S - LAST), slice(S - LAST, S)
-        for bank, js in zip(duo[2], halves):
+        for bank, js in zip(even, halves):
             nc.scalar.activation(out=h7[:, js], in_=first_product(1, 3, js, bank), func=ACT.Square)
         h_most = held([P, S - LAST], F32, "h_most", "raw10")
         nc.scalar.activation(out=h_most[:], in_=h7[:, most], func=ACT.Ln, bias=1.0)

@@ -244,6 +244,11 @@ def tile_list_cyclist_tile_page_kernel(
             out = planes.rearrange("p (u m e) -> p u m e", u=2, e=2)[:, t // 2, part, t % 2]
             copy_on(engine, out, page[g][t][:, cols])
 
+        def round_chunks(i, count):
+            g, t = tiles[i]
+            out = pairs[g][:].rearrange("p (c u m e) -> p c u m e", c=CHUNKS, u=2, e=2)[:, 0:count, t // 2, :, t % 2]
+            nc.scalar.copy(out=out, in_=page[g][t][:, 0 : BANK * count].rearrange("p (c m) -> p c m", m=BANK))
+
         def weave(engine, out, g, cols):
             planes, part = pair_planes(g, cols)
             words = planes.bitcast(U32).rearrange("p (u m) -> p m u", u=2)[:, part, :]
@@ -262,8 +267,8 @@ def tile_list_cyclist_tile_page_kernel(
         def store_scales(g):
             for q in range(QUADS):
                 nc.sync.dma_start(
-                    out=out_3[g, 4 * q : 4 * q + 4, :].bitcast(I32),
-                    in_=ps[g][32 * q : 32 * q + 4, :].bitcast(I32),
+                    out=out_3[g, q : 16 : QUADS, :].bitcast(I32),
+                    in_=ps[g][q:P:32, :].bitcast(I32),
                 )
 
         def factor(i, out, pair):
@@ -358,11 +363,9 @@ def tile_list_cyclist_tile_page_kernel(
         wbc = held([P, GROUPS * N], U32, "wbc", "raw10")
         nc.vector.quantize_mx(out=wbc[:].bitcast(FP8X4), scales=wbs[:], in_=wb_st)
         pairs.append(held([P, PACK * T2], BF16, "pairs1", "wide"))
-        for c in range(CHUNKS):
-            round_pair("scalar", 4, chunk(c))
+        round_chunks(4, CHUNKS)
         for i in (5, 6):
-            for c in range(CHUNKS - 1):
-                round_pair("scalar", i, chunk(c))
+            round_chunks(i, CHUNKS - 1)
         h_rest = held([P, LAST], F32, "h_rest", "raw11")
         nc.scalar.activation(out=h_rest[:], in_=h7[:, rest], func=ACT.Ln, bias=1.0)
         scatter(7, rest, h_rest[:])
@@ -393,27 +396,20 @@ def tile_list_cyclist_tile_page_kernel(
         y = [held([P, T2], F32, f"y{n}", f"raw0{n}") for n in range(N // P)]
         ya_sb = held([P, CHUNKS * BANK], F32, "ya_sb", "raw11")
 
-        def finish(c, n):
-            ya, yb = banks[4 * (c % 2) + 2 * n], banks[4 * (c % 2) + 2 * n + 1]
+        def keep_ya(c, n):
             at = (2 * c + n) % CHUNKS
-            kept = ya_sb[:, BANK * at : BANK * (at + 1)]
-            nc.scalar.copy(out=kept, in_=ya[:])
-            cols = slice(BANK * c, BANK * (c + 1))
-            nc.vector.tensor_tensor(out=y[n][:, cols], in0=yb[:], in1=kept, op=ALU.max)
-            nc.sync.dma_start(out=out_0[P * n : P * (n + 1), cols], in_=y[n][:, cols])
+            nc.scalar.copy(out=ya_sb[:, BANK * at : BANK * (at + 1)], in_=banks[4 * (c % 2) + 2 * n][:])
+
+        def larger(c, n):
+            at = (2 * c + n) % CHUNKS
+            yb = banks[4 * (c % 2) + 2 * n + 1]
+            nc.vector.tensor_tensor(out=y[n][:, chunk(c)], in0=yb[:], in1=ya_sb[:, BANK * at : BANK * (at + 1)], op=ALU.max)
+            nc.sync.dma_start(out=out_0[P * n : P * (n + 1), chunk(c)], in_=y[n][:, chunk(c)])
 
         for which in range(2):
             for c in range(2):
                 for n in range(N // P):
                     product(c, n, 0, which)
-
-        def close(c):
-            for which in range(2):
-                for n in range(N // P):
-                    for g in range(GROUPS) if c >= 2 else [1]:
-                        product(c, n, g, which)
-            for n in range(N // P):
-                finish(c, n)
 
         staged = [staging(f"st_last{pair}", pair) for pair in range(CHUNKS // 2)]
 
@@ -437,19 +433,41 @@ def tile_list_cyclist_tile_page_kernel(
             for which in range(2):
                 for n in range(N // P):
                     product(0, n, 1, which, cols.start, cols.stop)
+        rows = range(N // P)
         store_codes(1, chunk(0))
-        round_pair("vector", 7, chunk(2))
         last_planes(chunk(1))
         store_codes(1, chunk(1))
+        for which in range(2):
+            for n in rows:
+                product(1, n, 1, which)
+        round_pair("vector", 7, chunk(2))
         round_pair("scalar", 7, chunk(3))
         weave("vector", last_stage(chunk(2)), 1, chunk(2))
-        finish(0, 0)
         last_planes(chunk(2))
         store_codes(1, chunk(2))
-        finish(0, 1)
-        weave("scalar", last_stage(chunk(3)), 1, chunk(3))
+        weave("scalar", last_stage(halved(3)[0]), 1, halved(3)[0])
+        for n in rows:
+            keep_ya(0, n)
+        for g in range(GROUPS):
+            for n in rows:
+                product(2, n, g, 0)
+        for n in rows:
+            larger(0, n)
+            for g in range(GROUPS):
+                product(2, n, g, 1)
+        weave("scalar", last_stage(halved(3)[1]), 1, halved(3)[1])
         last_planes(chunk(3))
         store_codes(1, chunk(3))
         store_scales(1)
-        for c in range(1, CHUNKS):
-            close(c)
+        for n in rows:
+            keep_ya(1, n)
+            for g in range(GROUPS):
+                product(3, n, g, 0)
+        for n in rows:
+            larger(1, n)
+            for g in range(GROUPS):
+                product(3, n, g, 1)
+        for c in (2, 3):
+            for n in rows:
+                keep_ya(c, n)
+                larger(c, n)

@@ -60,12 +60,13 @@ def tile_list_cyclist_tile_page_kernel(
         page = [[held([P, T2], F32, f"page{g}{t}") for t in range(PACK)] for g in range(GROUPS)]
         w1c = [held([P, PASSES * KP], U32, f"w1c{g}") for g in range(GROUPS)]
         w1s = [held([P, PASSES * KP], U8, f"w1s{g}") for g in range(GROUPS)]
-        pc = [held([P, T2], U32, f"pc{g}") for g in range(GROUPS)]
+        WIDE = T2 // 2
+        pc = {(g, side): held([P, WIDE], U32, f"pc{g}{side}") for g in range(GROUPS) for side in range(2)}
         ps = [held([P, T2], U8, f"ps{g}") for g in range(GROUPS)]
         wbs = held([P, GROUPS * N], U8, "wbs")
         waw = held([P, GROUPS, 2 * N], U8, "waw")
         was = held([P, GROUPS, N], U8, "was")
-        pairs = [held([P, PACK * T2], BF16, "pairs0")]
+        pairs = [held([P, PACK * BANK], BF16, "pairs0")]
         warm = held([P, 2], F32, "warm")
 
         nc.vector.memset(tabs[32:64, :].bitcast(I32), 0)
@@ -83,10 +84,9 @@ def tile_list_cyclist_tile_page_kernel(
         page_out = out_1.rearrange("(g p t) c -> g t p c", g=GROUPS, t=PACK)
         w1_raw = {}
 
-        def load_words(a):
-            nc.sync.dma_start(
-                out=tabw[:, T * a : T * (a + 1)].bitcast(I32), in_=tab_words[a].rearrange("p n i -> p (n i)").bitcast(I32)
-            )
+        def load_words(a, lo=0, hi=T):
+            words = tab_words[a].rearrange("p n i -> p (n i)").bitcast(I32)
+            nc.sync.dma_start(out=tabw[:, T * a + lo : T * a + hi].bitcast(I32), in_=words[:, lo:hi])
 
         def load_w1(g, a, pieces=1):
             raw = held([P, PACK, KP], F32, f"w1raw{g}{a}", f"raw{g}{a}")
@@ -107,17 +107,18 @@ def tile_list_cyclist_tile_page_kernel(
             )
         wgs_sb = held([P, S], F32, "wgs_sb", "row0")
         nc.sync.dma_start(out=wgs_sb[:, 0:HALF], in_=wgs[:, 0:HALF])
-        nc.sync.dma_start(out=wgs_sb[:, HALF:S], in_=wgs[:, HALF:S])
+        load_words(0, 0, T // 2)
         nc.sync.dma_start(out=gain_sb[:], in_=gain.rearrange("(g p t) -> p g t", g=GROUPS, t=PACK))
-        load_words(0)
+        load_words(0, T // 2, T)
         nc.sync.dma_start(offs2_sb[:], offs2)
         load_w1(0, 0, 2)
         load_w1(0, 1, 2)
+        load_words(1)
         nc.vector.tensor_copy(out=picked[:], in_=tabs[:].indirect(offs_sb[:]))
         for q in range(QUADS):
             nc.sync.dma_start(out=vs[32 * q : 32 * q + 8, :].bitcast(I32), in_=picked[q:32:QUADS, :].bitcast(I32))
-        load_words(1)
         load_page(0, 0)
+        nc.sync.dma_start(out=wgs_sb[:, HALF:S], in_=wgs[:, HALF:S])
         load_page(0, 1)
         load_w1(1, 0)
         load_w1(1, 1)
@@ -163,32 +164,33 @@ def tile_list_cyclist_tile_page_kernel(
             )
 
         halves = [slice(0, HALF), slice(HALF, S)]
-        for b in range(S // BANK):
+        turned = (banks[0], banks[1], banks[6], banks[7])
+
+        def turn_wgs(b):
             for i in range(BANK // P):
                 lo = BANK * b + P * i
-                nc.tensor.transpose(banks[b][:, P * i : P * (i + 1)], wgs_sb[:, lo : lo + P], ident[:])
+                nc.tensor.transpose(turned[-1][:, P * i : P * (i + 1)], wgs_sb[:, lo : lo + P], ident[:])
 
         def spread_wgs(b, ts):
             blocks = spread[b][:, P // 2 : PACK * BANK + P // 2].rearrange("p (t i q m) -> p i t q m", t=PACK, q=QUADS, m=32)
-            rows = banks[b][:].rearrange("p (i m t) -> p i t m", t=PACK, m=32)
+            rows = turned[-1][:].rearrange("p (i m t) -> p i t m", t=PACK, m=32)
             nc.scalar.copy(
                 out=blocks[:, :, ts, 0:2, :],
                 in_=rows[:, :, ts].unsqueeze(3).to_broadcast([P, BANK // P, ts.stop - ts.start, 2, 32]),
             )
 
-        def turn_back(t, pair):
-            for b, bank in enumerate(pair):
-                for i in range(BANK // P):
-                    lo = BANK * t + P * i
-                    for shift in (0, P // 2):
-                        nc.tensor.matmul(
-                            bank[:, P * i : P * (i + 1)],
-                            lhsT=spread[b][:, lo + shift : lo + shift + P],
-                            rhs=ident[:],
-                            is_transpose=True,
-                            start=(shift == 0),
-                            stop=(shift != 0),
-                        )
+        def turn_back(b, t):
+            for i in range(BANK // P):
+                lo = BANK * t + P * i
+                for shift in (0, P // 2):
+                    nc.tensor.matmul(
+                        turned[t][:, P * i : P * (i + 1)],
+                        lhsT=spread[b][:, lo + shift : lo + shift + P],
+                        rhs=ident[:],
+                        is_transpose=True,
+                        start=(shift == 0),
+                        stop=(shift != 0),
+                    )
 
         def first_product(g, t, js, bank, order=(1, 0)):
             x = bank[:, 0 : js.stop - js.start]
@@ -207,8 +209,6 @@ def tile_list_cyclist_tile_page_kernel(
 
         tiles = [(g, t) for g in range(GROUPS) for t in range(PACK)]
         hs, factors = {}, {}
-
-        duo = [banks[2 * i : 2 * i + 2] for i in range(4)]
 
         def make_h(i, pair, h, squares=None):
             g, t = tiles[i]
@@ -234,9 +234,9 @@ def tile_list_cyclist_tile_page_kernel(
             nc.sync.dma_start(out=page_out[g, t], in_=page[g][t][:])
 
         def pair_planes(g, cols):
-            width = T2 if g == 0 else BANK
-            c, at = divmod(cols.start, width)
-            return pairs[g][:, PACK * width * c : PACK * width * (c + 1)], slice(at, at + cols.stop - cols.start)
+            c, at = divmod(cols.start, BANK)
+            c = c if g else 0
+            return pairs[g][:, PACK * BANK * c : PACK * BANK * (c + 1)], slice(at, at + cols.stop - cols.start)
 
         def round_pair(engine, i, cols):
             g, t = tiles[i]
@@ -257,12 +257,16 @@ def tile_list_cyclist_tile_page_kernel(
         def chunk(c):
             return slice(BANK * c, BANK * (c + 1))
 
+        def codes(g, cols):
+            side, at = divmod(cols.start, WIDE)
+            return pc[(g, side)][:, at : at + cols.stop - cols.start]
+
         def quantize_page(g, cols, in_):
-            nc.vector.quantize_mx(out=pc[g][:, cols].bitcast(FP8X4), scales=ps[g][:, cols], in_=in_)
+            nc.vector.quantize_mx(out=codes(g, cols).bitcast(FP8X4), scales=ps[g][:, cols], in_=in_)
 
         def store_codes(g, cols):
             words = out_2[g].rearrange("p m t -> p (m t)").bitcast(I32)
-            nc.sync.dma_start(out=words[:, cols], in_=pc[g][:, cols].bitcast(I32))
+            nc.sync.dma_start(out=words[:, cols], in_=codes(g, cols).bitcast(I32))
 
         def store_scales(g):
             for q in range(QUADS):
@@ -271,37 +275,50 @@ def tile_list_cyclist_tile_page_kernel(
                     in_=ps[g][q:P:32, :].bitcast(I32),
                 )
 
-        def factor(i, out, pair):
+        def factor(i, b):
             g, t = tiles[i]
-            factors[i] = out
-            for bank, js in zip(pair, halves):
-                nc.scalar.activation(out=out[:, js], in_=bank[:], func=ACT.Copy, scale=gain_sb[:, g, t : t + 1])
+            nc.scalar.activation(out=factors[i][:, halves[b]], in_=turned[t][:], func=ACT.Copy, scale=gain_sb[:, g, t : t + 1])
 
         whole = slice(0, S)
-        row = slice(0, T2)
+        left, right = slice(0, WIDE), slice(WIDE, T2)
+        beside = []
+
+        def lay_beside(t):
+            nc.sync.dma_start(out=beside[1][:, BANK * t : BANK * (t + 1)], in_=page[0][t][:, chunk(2)])
+            nc.sync.dma_start(out=beside[0][:, WIDE * t : WIDE * (t + 1)], in_=page[0][t][:, left])
+
+        def round_beside(c, out):
+            rows = beside[1 if c == 2 else 0][:].rearrange("p (j h c i) -> p h c j i", j=PACK, c=BANK // RUN, i=RUN)
+            nc.scalar.copy(out=out.rearrange("p (c i j) -> p c j i", i=RUN, j=PACK), in_=rows[:, c % 2])
 
         def place(i):
             scatter(i, whole, hs[i])
-            store_page(i)
+            if i < PACK:
+                lay_beside(i)
+            else:
+                store_page(i)
 
         def fresh(name, tag):
             return held([P, S], F32, name, tag)[:]
 
         gather_words(0, whole)
+        turn_wgs(0)
         for ts in (slice(0, 1), slice(1, PACK)):
-            for b in range(S // BANK):
-                spread_wgs(b, ts)
+            spread_wgs(0, ts)
         st_w = staging("st_w0", 0)
         for a in range(PASSES):
             cast_w1(0, a, st_w, ["vector"])
             quantize_w1(0, st_w, a, a + 1)
         early = held([P, 2 * S], F32, "early")
         late = held([P, 2 * S], F32, "late", "raw00")
-        second = (early[:, 0:S], late[:, 0:S], late[:, S : 2 * S])
-        for t, pair, tag in ((0, duo[1], "row1"), (1, duo[0], "row2"), (2, duo[3], "row0")):
-            turn_back(t, pair)
-            factor(t, fresh(f"factor{t}", tag), pair)
-            factor(PACK + t, second[t], pair)
+        for t, tag in enumerate(("row1", "row2", "row5", "row6")):
+            factors[t] = fresh(f"factor{t}", tag)
+        for t, rows in enumerate((early[:, 0:S], late[:, 0:S], late[:, S : 2 * S], early[:, S : 2 * S])):
+            factors[PACK + t] = rows
+        for t in range(PACK):
+            turn_back(0, t)
+        for i in (0, 1, 2, 3, 4, 7, 5, 6):
+            factor(i, 0)
         first_pieces = [slice(0, S // 4), slice(S // 4, HALF), slice(HALF, S)]
         for js in first_pieces:
             gather_words(1, js)
@@ -309,47 +326,58 @@ def tile_list_cyclist_tile_page_kernel(
         def lent(slot):
             return pairs[0][:].bitcast(F32)[:, S * slot : S * (slot + 1)]
 
-        h0 = fresh("h0", "row3")
-        for bank, js in zip((banks[4], banks[3], banks[2]), first_pieces):
-            squares = lent(0)[:, S // 4 : S // 4 + js.stop - js.start]
-            nc.scalar.activation(out=squares, in_=first_product(0, 0, js, bank, (0, 1)), func=ACT.Square)
-            nc.scalar.activation(out=h0[:, js], in_=squares, func=ACT.Ln, bias=1.0)
-            scatter(0, js, h0[:, js])
-        store_page(0)
+        def piece(i, js, bank, h):
+            squares = lent(0)[:, 0 : js.stop - js.start]
+            nc.scalar.activation(out=squares, in_=first_product(0, i, js, bank, (0, 1)), func=ACT.Square)
+            nc.scalar.activation(out=h[:, js], in_=squares, func=ACT.Ln, bias=1.0)
 
         def stream(i, pair, h, squares=None):
             make_h(i, pair, h, squares)
             place(i)
 
-        odd, even = (banks[5], banks[4]), (banks[3], banks[2])
-        stream(1, odd, fresh("h1", "row4"), lent(0))
+        h0, h1 = fresh("h0", "row3"), fresh("h1", "row4")
+        for i, js, bank, h in ((0, first_pieces[0], banks[2], h0), (0, first_pieces[1], banks[3], h0), (1, halves[0], banks[4], h1)):
+            piece(i, js, bank, h)
+            scatter(i, js, h[:, js])
+        piece(0, halves[1], banks[5], h0)
+        piece(1, halves[1], banks[2], h1)
+        turn_wgs(1)
+        for ts in (slice(0, 1), slice(1, PACK)):
+            spread_wgs(1, ts)
+        beside.append(held([P, PACK * WIDE], F32, "beside01", "wide"))
+        beside.append(held([P, PACK * BANK], F32, "beside2", "spread0"))
+        for t, h in enumerate((h0, h1)):
+            turn_back(1, t)
+            factor(t, 1)
+            scatter(t, halves[1], h[:, halves[1]])
+            lay_beside(t)
+        odd, even = (banks[5], banks[2]), (banks[3], banks[4])
         st_w = staging("st_w1", 1)
         cast_w1(1, 0, st_w, ["scalar"])
+        turn_back(1, 2)
+        factor(2, 1)
         stream(2, even, fresh("h2", "row1"), lent(0))
-        turn_back(3, odd)
-        factor(3, fresh("factor3", "row3"), odd)
-        factor(7, early[:, S : 2 * S], odd)
+        turn_back(1, 3)
         cast_w1(1, 1, st_w, ["scalar"])
         quantize_w1(1, st_w, 0, PASSES)
-        stream(3, even, held([P, S], F32, "h3", "raw10")[:])
-        round_pair("scalar", 0, row)
-        round_pair("scalar", 1, row)
-        stream(4, odd, fresh("h4", "row2"), lent(2))
-        stream(5, even, fresh("h5", "row4"))
-        round_pair("scalar", 2, row)
-        stream(6, odd, held([P, S], F32, "h6", "raw11")[:])
-        round_pair("scalar", 3, row)
-        for pair in range(CHUNKS // 2):
-            st = staging(f"st_p{pair}", pair)
-            cols = slice(2 * BANK * pair, 2 * BANK * (pair + 1))
-            weave("scalar", st[:], 0, cols)
-            quantize_page(0, cols, st[:])
-        store_codes(0, slice(0, T2))
-        store_scales(0)
+        factor(3, 1)
+        stream(3, odd, held([P, S], F32, "h3", "raw10")[:])
+        for t in range(PACK):
+            factor(PACK + t, 1)
+        for i in range(PACK):
+            store_page(i)
+        for i in range(PACK - 1):
+            round_pair("scalar", i, chunk(3))
+        stream(4, even, fresh("h4", "row2"))
+        stream(5, odd, fresh("h5", "row4"))
+        round_pair("scalar", 3, chunk(3))
+        st_right = staging("st_right", 1)
+        weave("scalar", st_right[:, PACK * BANK : 2 * PACK * BANK], 0, chunk(3))
+        stream(6, even, held([P, S], F32, "h6", "raw11")[:])
 
-        h7 = held([P, S], F32, "h7", "spread0")
+        h7 = held([P, S], F32, "h7", "spread1")
         most, rest = slice(0, S - LAST), slice(S - LAST, S)
-        for bank, js in zip(even, halves):
+        for bank, js in zip(odd, halves):
             nc.scalar.activation(out=h7[:, js], in_=first_product(1, 3, js, bank), func=ACT.Square)
         h_most = held([P, S - LAST], F32, "h_most", "raw10")
         nc.scalar.activation(out=h_most[:], in_=h7[:, most], func=ACT.Ln, bias=1.0)
@@ -360,13 +388,23 @@ def tile_list_cyclist_tile_page_kernel(
                 out=wb_st[:, g * PACK * N : (g + 1) * PACK * N].rearrange("p (c i j) -> p c j i", i=RUN, j=PACK),
                 in_=wb_raw[:, g, :].rearrange("p (j c i) -> p c j i", i=RUN, j=PACK),
             )
-        wbc = held([P, GROUPS * N], U32, "wbc", "raw10")
+        wbc = held([P, GROUPS * N], U32, "wbc", "row3")
         nc.vector.quantize_mx(out=wbc[:].bitcast(FP8X4), scales=wbs[:], in_=wb_st)
-        pairs.append(held([P, PACK * T2], BF16, "pairs1", "wide"))
+        round_beside(2, st_right[:, 0 : PACK * BANK])
+        quantize_page(0, right, st_right[:])
+        store_codes(0, right)
+        st_left = staging("st_left", 0)
+        for c in range(2):
+            round_beside(c, st_left[:, PACK * BANK * c : PACK * BANK * (c + 1)])
+        quantize_page(0, left, st_left[:])
+        store_codes(0, left)
+        store_scales(0)
+        wide = held([P, PACK * T2 + 2 * LAST], BF16, "pairs1", "wide")
+        pairs.append(wide[:, 0 : PACK * T2])
         round_chunks(4, CHUNKS)
         for i in (5, 6):
             round_chunks(i, CHUNKS - 1)
-        h_rest = held([P, LAST], F32, "h_rest", "raw11")
+        h_rest = wide[:, PACK * T2 : PACK * T2 + 2 * LAST].bitcast(F32)
         nc.scalar.activation(out=h_rest[:], in_=h7[:, rest], func=ACT.Ln, bias=1.0)
         scatter(7, rest, h_rest[:])
         for i in (5, 6):
@@ -387,7 +425,7 @@ def tile_list_cyclist_tile_page_kernel(
                 out=bank[:, lo:hi],
                 lhsT=lhsT,
                 lhsT_scale=lhsT_scale,
-                rhs=pc[g][:, cols].bitcast(FP8X4),
+                rhs=codes(g, cols).bitcast(FP8X4),
                 rhs_scale=ps[g][:, cols],
                 start=(g == 0),
                 stop=(g == GROUPS - 1 and hi == BANK),
@@ -411,7 +449,7 @@ def tile_list_cyclist_tile_page_kernel(
                 for n in range(N // P):
                     product(c, n, 0, which)
 
-        staged = [staging(f"st_last{pair}", pair) for pair in range(CHUNKS // 2)]
+        staged = [staging("st_last0", 0), staging("st_last1", 1)]
 
         def last_stage(cols):
             at = cols.start % (2 * BANK)

from contextlib import ExitStack

import concourse.mybir as mybir
from concourse.masks import make_identity

K, H, N, T, S, T2 = 1024, 1024, 256, 2048, 1024, 2048
FLOPS = 2 * K * H * S + 2 * 2 * H * N * T2

F32 = mybir.dt.float32
BF16 = mybir.dt.bfloat16
I32 = mybir.dt.int32
U32 = mybir.dt.uint32
U16 = mybir.dt.uint16
U8 = mybir.dt.uint8
FP8X4 = mybir.dt.float8_e4m3fn_x4
FP4X4 = mybir.dt.float4_e2m1fn_x4
ACT = mybir.ActivationFunctionType
ALU = mybir.AluOpType

P = 128
PACK = 4
KP = P * PACK
BANK = 512
PASSES = K // KP
GROUPS = H // KP
CHUNKS = T2 // BANK
QUADS = 4
HALF = S // 2
RUN = 4
LAST = 256


def tile_list_cyclist_tile_page_kernel(
    tc, tab_words, tab_scales, offs, w1, gain, page0, offs2, wgs, wa4_words, wa4_scales, wb,
    out_0, out_1, out_2, out_3,
):
    nc = tc.nc
    with ExitStack() as ctx:
        keep = ctx.enter_context(tc.tile_pool(name="keep", bufs=1))
        psum = ctx.enter_context(tc.psum_pool(name="psum", bufs=1))

        def held(shape, dtype, name, tag=None):
            return keep.tile(shape, dtype, name=name, tag=tag or name, align_bytes=64)

        def staging(name, turn):
            return held([P, 2 * PACK * BANK], BF16, name, f"stage{turn}")

        banks = [psum.tile([P, BANK], F32, name=f"bank{b}") for b in range(8)]

        offs_sb = keep.tile([P, S // 16], U16, name="offs_sb")
        offs2_sb = keep.tile([P, S // 16], U16, name="offs2_sb")
        tabw = held([P, PASSES * T], U32, "tabw", "wide")
        tabs = held([P, T], U8, "tabs")
        vw = [held([P, S], U32, f"vw{a}") for a in range(PASSES)]
        picked = held([P, S], U8, "picked")
        vs = held([P, S], U8, "vs")
        gain_sb = held([P, GROUPS, PACK], F32, "gain_sb")
        spread = [held([P, PACK * BANK + P // 2], F32, f"spread{b}") for b in range(S // BANK)]
        ident = held([P, P], F32, "ident")
        page = [[held([P, T2], F32, f"page{g}{t}") for t in range(PACK)] for g in range(GROUPS)]
        w1c = [held([P, PASSES * KP], U32, f"w1c{g}") for g in range(GROUPS)]
        w1s = [held([P, PASSES * KP], U8, f"w1s{g}") for g in range(GROUPS)]
        WIDE = T2 // 2
        pc = {(g, side): held([P, WIDE], U32, f"pc{g}{side}") for g in range(GROUPS) for side in range(2)}
        ps = [held([P, T2], U8, f"ps{g}") for g in range(GROUPS)]
        wbs = held([P, GROUPS * N], U8, "wbs")
        waw = held([P, GROUPS, 2 * N], U8, "waw")
        was = held([P, GROUPS, N], U8, "was")
        pairs = [held([P, PACK * BANK], BF16, "pairs0")]
        warm = held([P, 2], F32, "warm")

        nc.vector.memset(tabs[32:64, :].bitcast(I32), 0)
        nc.vector.memset(tabs[64:P, :].bitcast(I32), 0)
        nc.vector.memset(warm[:, 0:1], 1.0)
        nc.scalar.activation(out=warm[:, 1:2], in_=warm[:, 0:1], func=ACT.Ln)
        make_identity(nc, ident[:])
        nc.gpsimd.memset(vs[:].bitcast(I32), 0)
        for rows in spread:
            nc.gpsimd.memset(rows[:, 0 : PACK * BANK].rearrange("p (i c) -> p i c", c=P)[:, :, 0 : P // 2], 0.0)
            nc.gpsimd.memset(rows[:, PACK * BANK : PACK * BANK + P // 2], 0.0)
        nc.gpsimd.memset(was[:].rearrange("p g n -> p (g n)").bitcast(I32), 0)

        page_in = page0.rearrange("(g p t) c -> g t p c", g=GROUPS, t=PACK)
        page_out = out_1.rearrange("(g p t) c -> g t p c", g=GROUPS, t=PACK)
        w1_raw = {}

        def load_words(a, lo=0, hi=T):
            words = tab_words[a].rearrange("p n i -> p (n i)").bitcast(I32)
            nc.sync.dma_start(out=tabw[:, T * a + lo : T * a + hi].bitcast(I32), in_=words[:, lo:hi])

        def load_w1(g, a, pieces=1):
            raw = held([P, PACK, KP], F32, f"w1raw{g}{a}", f"raw{g}{a}")
            rows = w1[KP * a : KP * (a + 1), KP * g : KP * (g + 1)].rearrange("(p j) c -> p j c", j=PACK)
            for i in range(pieces):
                slots = slice(PACK // pieces * i, PACK // pieces * (i + 1))
                nc.sync.dma_start(out=raw[:, slots, :], in_=rows[:, slots, :])
            w1_raw[(g, a)] = raw

        def load_page(g, t):
            nc.sync.dma_start(out=page[g][t][:], in_=page_in[g, t])

        nc.sync.dma_start(offs_sb[:], offs)
        for a in range(PASSES):
            nc.sync.dma_start(
                out=tabs[16 * a : 16 * (a + 1), :].bitcast(I32),
                in_=tab_scales[a].rearrange("(q r) c -> r q c", q=QUADS).bitcast(I32),
            )
        wgs_sb = held([P, S], F32, "wgs_sb", "row0")
        nc.sync.dma_start(out=wgs_sb[:, 0:HALF], in_=wgs[:, 0:HALF])
        load_words(0, 0, T // 2)
        nc.sync.dma_start(out=gain_sb[:], in_=gain.rearrange("(g p t) -> p g t", g=GROUPS, t=PACK))
        load_words(0, T // 2, T)
        nc.sync.dma_start(offs2_sb[:], offs2)
        load_w1(0, 0, 2)
        load_w1(0, 1, 2)
        load_words(1)
        nc.vector.tensor_copy(out=picked[:], in_=tabs[:].indirect(offs_sb[:]))
        for q in range(QUADS):
            nc.sync.dma_start(out=vs[32 * q : 32 * q + 8, :].bitcast(I32), in_=picked[q:32:QUADS, :].bitcast(I32))
        load_page(0, 0)
        nc.sync.dma_start(out=wgs_sb[:, HALF:S], in_=wgs[:, HALF:S])
        load_page(0, 1)
        load_w1(1, 0)
        load_w1(1, 1)
        load_page(0, 2)
        load_page(0, 3)
        nc.sync.dma_start(out=waw[:].bitcast(I32), in_=wa4_words.rearrange("g p c -> p g c").bitcast(I32))
        for q in range(QUADS):
            nc.sync.dma_start(
                out=was[32 * q : 32 * q + 4, :, :].bitcast(I32),
                in_=wa4_scales[:, 4 * q : 4 * q + 4, :].rearrange("g r n -> r g n").bitcast(I32),
            )
        for t in range(PACK):
            load_page(1, t)
        wb_raw = held([P, GROUPS, PACK * N], F32, "wb_raw", "raw01")
        nc.sync.dma_start(out=wb_raw[:], in_=wb.rearrange("(g p j) n -> p g (j n)", g=GROUPS, j=PACK))

        def copy_on(engine, out, in_):
            if engine == "vector":
                nc.vector.tensor_copy(out=out, in_=in_)
            else:
                nc.scalar.copy(out=out, in_=in_)

        def cast_w1(g, a, st, engines):
            part = st[:, PACK * KP * a : PACK * KP * (a + 1)]
            share = PACK // len(engines)
            for i, engine in enumerate(engines):
                ts = slice(share * i, share * (i + 1))
                copy_on(
                    engine,
                    part.rearrange("p (t m j) -> p m j t", t=PACK, j=PACK)[:, :, :, ts],
                    w1_raw[(g, a)][:].rearrange("p j (m t) -> p m j t", t=PACK)[:, :, :, ts],
                )

        def quantize_w1(g, st, lo, hi):
            cols = slice(KP * lo, KP * hi)
            nc.vector.quantize_mx(
                out=w1c[g][:, cols].bitcast(FP8X4), scales=w1s[g][:, cols], in_=st[:, PACK * KP * lo : PACK * KP * hi]
            )

        def gather_words(a, js):
            nc.vector.tensor_copy(
                out=vw[a][:, js], in_=tabw[:, T * a : T * (a + 1)].indirect(offs_sb[:, js.start // 16 : js.stop // 16])
            )

        halves = [slice(0, HALF), slice(HALF, S)]
        turned = (banks[0], banks[1], banks[6], banks[7])

        def turn_wgs(b):
            for i in range(BANK // P):
                lo = BANK * b + P * i
                nc.tensor.transpose(turned[-1][:, P * i : P * (i + 1)], wgs_sb[:, lo : lo + P], ident[:])

        def spread_wgs(b, ts):
            blocks = spread[b][:, P // 2 : PACK * BANK + P // 2].rearrange("p (t i q m) -> p i t q m", t=PACK, q=QUADS, m=32)
            rows = turned[-1][:].rearrange("p (i m t) -> p i t m", t=PACK, m=32)
            nc.scalar.copy(
                out=blocks[:, :, ts, 0:2, :],
                in_=rows[:, :, ts].unsqueeze(3).to_broadcast([P, BANK // P, ts.stop - ts.start, 2, 32]),
            )

        def turn_back(b, t):
            for i in range(BANK // P):
                lo = BANK * t + P * i
                for shift in (0, P // 2):
                    nc.tensor.matmul(
                        turned[t][:, P * i : P * (i + 1)],
                        lhsT=spread[b][:, lo + shift : lo + shift + P],
                        rhs=ident[:],
                        is_transpose=True,
                        start=(shift == 0),
                        stop=(shift != 0),
                    )

        def first_product(g, t, js, bank, order=(1, 0)):
            x = bank[:, 0 : js.stop - js.start]
            for a in order:
                cols = slice(KP * a + P * t, KP * a + P * (t + 1))
                nc.tensor.matmul_mx(
                    out=x,
                    lhsT=w1c[g][:, cols].bitcast(FP8X4),
                    lhsT_scale=w1s[g][:, cols],
                    rhs=vw[a][:, js].bitcast(FP8X4),
                    rhs_scale=vs[4 * a : P, js],
                    start=(a == order[0]),
                    stop=(a == order[-1]),
                )
            return x

        tiles = [(g, t) for g in range(GROUPS) for t in range(PACK)]
        hs, factors = {}, {}

        def make_h(i, pair, h, squares=None):
            g, t = tiles[i]
            squares = h if squares is None else squares
            xs = [first_product(g, t, js, bank) for bank, js in zip(pair, halves)]
            for x, js in zip(xs, halves):
                nc.scalar.activation(out=squares[:, js], in_=x, func=ACT.Square)
            for js in halves:
                nc.scalar.activation(out=h[:, js], in_=squares[:, js], func=ACT.Ln, bias=1.0)
            hs[i] = h

        def scatter(i, js, values):
            g, t = tiles[i]
            nc.vector.tensor_tensor(
                out=page[g][t][:].indirect(offs2_sb[:, js.start // 16 : js.stop // 16]),
                in0=values,
                in1=factors[i][:, js],
                op=ALU.mult,
            )

        def store_page(i):
            g, t = tiles[i]
            nc.sync.dma_start(out=page_out[g, t], in_=page[g][t][:])

        def pair_planes(g, cols):
            c, at = divmod(cols.start, BANK)
            c = c if g else 0
            return pairs[g][:, PACK * BANK * c : PACK * BANK * (c + 1)], slice(at, at + cols.stop - cols.start)

        def round_pair(engine, i, cols):
            g, t = tiles[i]
            planes, part = pair_planes(g, cols)
            out = planes.rearrange("p (u m e) -> p u m e", u=2, e=2)[:, t // 2, part, t % 2]
            copy_on(engine, out, page[g][t][:, cols])

        def round_chunks(i, count):
            g, t = tiles[i]
            out = pairs[g][:].rearrange("p (c u m e) -> p c u m e", c=CHUNKS, u=2, e=2)[:, 0:count, t // 2, :, t % 2]
            nc.scalar.copy(out=out, in_=page[g][t][:, 0 : BANK * count].rearrange("p (c m) -> p c m", m=BANK))

        def weave(engine, out, g, cols):
            planes, part = pair_planes(g, cols)
            words = planes.bitcast(U32).rearrange("p (u m) -> p m u", u=2)[:, part, :]
            copy_on(engine, out.bitcast(U32).rearrange("p (m u) -> p m u", u=2), words)

        def chunk(c):
            return slice(BANK * c, BANK * (c + 1))

        def codes(g, cols):
            side, at = divmod(cols.start, WIDE)
            return pc[(g, side)][:, at : at + cols.stop - cols.start]

        def quantize_page(g, cols, in_):
            nc.vector.quantize_mx(out=codes(g, cols).bitcast(FP8X4), scales=ps[g][:, cols], in_=in_)

        def store_codes(g, cols):
            words = out_2[g].rearrange("p m t -> p (m t)").bitcast(I32)
            nc.sync.dma_start(out=words[:, cols], in_=codes(g, cols).bitcast(I32))

        def store_scales(g):
            for q in range(QUADS):
                nc.sync.dma_start(
                    out=out_3[g, q : 16 : QUADS, :].bitcast(I32),
                    in_=ps[g][q:P:32, :].bitcast(I32),
                )

        def factor(i, b):
            g, t = tiles[i]
            nc.scalar.activation(out=factors[i][:, halves[b]], in_=turned[t][:], func=ACT.Copy, scale=gain_sb[:, g, t : t + 1])

        whole = slice(0, S)
        left, right = slice(0, WIDE), slice(WIDE, T2)
        beside = []

        def lay_beside(t):
            nc.sync.dma_start(out=beside[1][:, BANK * t : BANK * (t + 1)], in_=page[0][t][:, chunk(2)])
            nc.sync.dma_start(out=beside[0][:, WIDE * t : WIDE * (t + 1)], in_=page[0][t][:, left])

        def round_beside(c, out):
            rows = beside[1 if c == 2 else 0][:].rearrange("p (j h c i) -> p h c j i", j=PACK, c=BANK // RUN, i=RUN)
            nc.scalar.copy(out=out.rearrange("p (c i j) -> p c j i", i=RUN, j=PACK), in_=rows[:, c % 2])

        def place(i):
            scatter(i, whole, hs[i])
            if i < PACK:
                lay_beside(i)
            else:
                store_page(i)

        def fresh(name, tag):
            return held([P, S], F32, name, tag)[:]

        gather_words(0, whole)
        turn_wgs(0)
        for ts in (slice(0, 1), slice(1, PACK)):
            spread_wgs(0, ts)
        st_w = staging("st_w0", 0)
        for a in range(PASSES):
            cast_w1(0, a, st_w, ["vector"])
            quantize_w1(0, st_w, a, a + 1)
        early = held([P, 2 * S], F32, "early")
        late = held([P, 2 * S], F32, "late", "raw00")
        for t, tag in enumerate(("row1", "row2", "row5", "row6")):
            factors[t] = fresh(f"factor{t}", tag)
        for t, rows in enumerate((early[:, 0:S], late[:, 0:S], late[:, S : 2 * S], early[:, S : 2 * S])):
            factors[PACK + t] = rows
        for t in range(PACK):
            turn_back(0, t)
        for i in (0, 1, 2, 3, 4, 7, 5, 6):
            factor(i, 0)
        first_pieces = [slice(0, S // 4), slice(S // 4, HALF), slice(HALF, S)]
        for js in first_pieces:
            gather_words(1, js)

        def lent(slot):
            return pairs[0][:].bitcast(F32)[:, S * slot : S * (slot + 1)]

        def piece(i, js, bank, h):
            squares = lent(0)[:, 0 : js.stop - js.start]
            nc.scalar.activation(out=squares, in_=first_product(0, i, js, bank, (0, 1)), func=ACT.Square)
            nc.scalar.activation(out=h[:, js], in_=squares, func=ACT.Ln, bias=1.0)

        def stream(i, pair, h, squares=None):
            make_h(i, pair, h, squares)
            place(i)

        h0, h1 = fresh("h0", "row3"), fresh("h1", "row4")
        for i, js, bank, h in ((0, first_pieces[0], banks[2], h0), (0, first_pieces[1], banks[3], h0), (1, halves[0], banks[4], h1)):
            piece(i, js, bank, h)
            scatter(i, js, h[:, js])
        piece(0, halves[1], banks[5], h0)
        piece(1, halves[1], banks[2], h1)
        turn_wgs(1)
        for ts in (slice(0, 1), slice(1, PACK)):
            spread_wgs(1, ts)
        beside.append(held([P, PACK * WIDE], F32, "beside01", "wide"))
        beside.append(held([P, PACK * BANK], F32, "beside2", "spread0"))
        for t, h in enumerate((h0, h1)):
            turn_back(1, t)
            factor(t, 1)
            scatter(t, halves[1], h[:, halves[1]])
            lay_beside(t)
        odd, even = (banks[5], banks[2]), (banks[3], banks[4])
        st_w = staging("st_w1", 1)
        cast_w1(1, 0, st_w, ["scalar"])
        turn_back(1, 2)
        factor(2, 1)
        stream(2, even, fresh("h2", "row1"), lent(0))
        turn_back(1, 3)
        cast_w1(1, 1, st_w, ["scalar"])
        quantize_w1(1, st_w, 0, PASSES)
        factor(3, 1)
        stream(3, odd, held([P, S], F32, "h3", "raw10")[:])
        for t in range(PACK):
            factor(PACK + t, 1)
        for i in range(PACK):
            store_page(i)
        for i in range(PACK - 1):
            round_pair("scalar", i, chunk(3))
        stream(4, even, fresh("h4", "row2"))
        stream(5, odd, fresh("h5", "row4"))
        round_pair("scalar", 3, chunk(3))
        st_right = staging("st_right", 1)
        weave("scalar", st_right[:, PACK * BANK : 2 * PACK * BANK], 0, chunk(3))
        stream(6, even, held([P, S], F32, "h6", "raw11")[:])

        h7 = held([P, S], F32, "h7", "spread1")
        most, rest = slice(0, S - LAST), slice(S - LAST, S)
        for bank, js in zip(odd, halves):
            nc.scalar.activation(out=h7[:, js], in_=first_product(1, 3, js, bank), func=ACT.Square)
        h_most = held([P, S - LAST], F32, "h_most", "raw10")
        nc.scalar.activation(out=h_most[:], in_=h7[:, most], func=ACT.Ln, bias=1.0)
        scatter(7, most, h_most[:])
        wb_st = fresh("wb_st", "row0").bitcast(BF16)
        for g in range(GROUPS):
            nc.scalar.copy(
                out=wb_st[:, g * PACK * N : (g + 1) * PACK * N].rearrange("p (c i j) -> p c j i", i=RUN, j=PACK),
                in_=wb_raw[:, g, :].rearrange("p (j c i) -> p c j i", i=RUN, j=PACK),
            )
        wbc = held([P, GROUPS * N], U32, "wbc", "row3")
        nc.vector.quantize_mx(out=wbc[:].bitcast(FP8X4), scales=wbs[:], in_=wb_st)
        round_beside(2, st_right[:, 0 : PACK * BANK])
        quantize_page(0, right, st_right[:])
        store_codes(0, right)
        st_left = staging("st_left", 0)
        for c in range(2):
            round_beside(c, st_left[:, PACK * BANK * c : PACK * BANK * (c + 1)])
        quantize_page(0, left, st_left[:])
        store_codes(0, left)
        store_scales(0)
        wide = held([P, PACK * T2 + 2 * LAST], BF16, "pairs1", "wide")
        pairs.append(wide[:, 0 : PACK * T2])
        round_chunks(4, CHUNKS)
        for i in (5, 6):
            round_chunks(i, CHUNKS - 1)
        h_rest = wide[:, PACK * T2 : PACK * T2 + 2 * LAST].bitcast(F32)
        nc.scalar.activation(out=h_rest[:], in_=h7[:, rest], func=ACT.Ln, bias=1.0)
        scatter(7, rest, h_rest[:])
        for i in (5, 6):
            round_pair("scalar", i, chunk(CHUNKS - 1))
        store_page(7)

        def product(c, n, g, which, lo=0, hi=BANK):
            cols = slice(BANK * c + lo, BANK * c + hi)
            bank = banks[4 * (c % 2) + 2 * n + which]
            if which == 0:
                lhsT = waw[:, g, 2 * P * n : 2 * P * (n + 1)].bitcast(FP4X4)
                lhsT_scale = was[:, g, P * n : P * (n + 1)]
            else:
                wcols = slice(N * g + P * n, N * g + P * (n + 1))
                lhsT = wbc[:, wcols].bitcast(FP8X4)
                lhsT_scale = wbs[:, wcols]
            nc.tensor.matmul_mx(
                out=bank[:, lo:hi],
                lhsT=lhsT,
                lhsT_scale=lhsT_scale,
                rhs=codes(g, cols).bitcast(FP8X4),
                rhs_scale=ps[g][:, cols],
                start=(g == 0),
                stop=(g == GROUPS - 1 and hi == BANK),
            )

        y = [held([P, T2], F32, f"y{n}", f"raw0{n}") for n in range(N // P)]
        ya_sb = held([P, CHUNKS * BANK], F32, "ya_sb", "raw11")

        def keep_ya(c, n):
            at = (2 * c + n) % CHUNKS
            nc.scalar.copy(out=ya_sb[:, BANK * at : BANK * (at + 1)], in_=banks[4 * (c % 2) + 2 * n][:])

        def larger(c, n):
            at = (2 * c + n) % CHUNKS
            yb = banks[4 * (c % 2) + 2 * n + 1]
            nc.vector.tensor_tensor(out=y[n][:, chunk(c)], in0=yb[:], in1=ya_sb[:, BANK * at : BANK * (at + 1)], op=ALU.max)
            nc.sync.dma_start(out=out_0[P * n : P * (n + 1), chunk(c)], in_=y[n][:, chunk(c)])

        for which in range(2):
            for c in range(2):
                for n in range(N // P):
                    product(c, n, 0, which)

        staged = [staging("st_last0", 0), staging("st_last1", 1)]

        def last_stage(cols):
            at = cols.start % (2 * BANK)
            return staged[cols.start // (2 * BANK)][:, PACK * at : PACK * (at + cols.stop - cols.start)]

        def last_planes(cols):
            quantize_page(1, cols, last_stage(cols))

        def halved(c):
            return [slice(BANK * c, BANK * c + BANK // 2), slice(BANK * c + BANK // 2, BANK * (c + 1))]

        for engine, c in (("vector", 0), ("scalar", 1)):
            for cols in halved(c):
                round_pair(engine, 7, cols)
            for cols in halved(c):
                weave(engine, last_stage(cols), 1, cols)
        for cols in halved(0):
            last_planes(cols)
            for which in range(2):
                for n in range(N // P):
                    product(0, n, 1, which, cols.start, cols.stop)
        rows = range(N // P)
        store_codes(1, chunk(0))
        last_planes(chunk(1))
        store_codes(1, chunk(1))
        for which in range(2):
            for n in rows:
                product(1, n, 1, which)
        round_pair("vector", 7, chunk(2))
        round_pair("scalar", 7, chunk(3))
        weave("vector", last_stage(chunk(2)), 1, chunk(2))
        last_planes(chunk(2))
        store_codes(1, chunk(2))
        weave("scalar", last_stage(halved(3)[0]), 1, halved(3)[0])
        for n in rows:
            keep_ya(0, n)
        for g in range(GROUPS):
            for n in rows:
                product(2, n, g, 0)
        for n in rows:
            larger(0, n)
            for g in range(GROUPS):
                product(2, n, g, 1)
        weave("scalar", last_stage(halved(3)[1]), 1, halved(3)[1])
        last_planes(chunk(3))
        store_codes(1, chunk(3))
        store_scales(1)
        for n in rows:
            keep_ya(1, n)
            for g in range(GROUPS):
                product(3, n, g, 0)
        for n in rows:
            larger(1, n)
            for g in range(GROUPS):
                product(3, n, g, 1)
        for c in (2, 3):
            for n in rows:
                keep_ya(c, n)
                larger(c, n)
